import numpy as np
import ml_dtypes


def mxq(x, axis, fmt="e4m3"):
    dtype, down = {"e4m3": (ml_dtypes.float8_e4m3fn, 7), "e5m2": (ml_dtypes.float8_e5m2, 14)}[fmt]
    v = np.moveaxis(np.asarray(x, np.float32).astype(ml_dtypes.bfloat16).astype(np.float64), axis, -1)
    blocks = v.reshape(v.shape[:-1] + (-1, 32))
    amax = np.abs(blocks).max(-1, keepdims=True)
    byte = np.maximum(np.where(amax > 0, np.frexp(amax)[1] - 1 + 127, 0) - down, 1)
    scale = np.exp2(byte - 127.0)
    codes = (blocks / scale).astype(np.float32).astype(dtype).astype(np.float64)
    return np.moveaxis((codes * scale).reshape(v.shape), -1, axis)


WIDE = False


def mx_kscale(k):
    if not WIDE:
        return np.ones(k)
    levels = np.array([10, -10, 5, -5, 0])
    if k % 512:
        return np.exp2(np.random.permutation(np.resize(levels, k // 32))).repeat(32)
    a = np.empty((k // 512, 16))
    for p in range(k // 512):
        a[p, :8] = np.random.permutation(np.resize(levels, 8))
        for g in range(8):
            far = levels[np.abs(levels - a[p, g]) >= 10]
            a[p, g + 8] = far[np.random.randint(len(far))]
    return np.exp2(a.ravel()).repeat(32)


def f64(x):
    return np.asarray(x).astype(np.float64)


def striped(idx):
    return np.tile(idx.reshape(-1, 16).T, (8, 1)).astype(np.uint16)


def unstriped(offs):
    return offs[:16].T.reshape(-1).astype(np.int64)


E2M1 = np.array([0.0, 0.5, 1.0, 1.5, 2.0, 3.0, 4.0, 6.0, -0.0, -0.5, -1.0, -1.5, -2.0, -3.0, -4.0, -6.0])


def pack_weight(w, fmt):
    k, n = w.shape
    w = f64(np.asarray(w, np.float32).astype(ml_dtypes.bfloat16)).reshape(k // 32, 32, n)
    amax = np.abs(w).max(1)
    if fmt == "e4m3":
        byte = np.frexp(amax)[1] - 1 + 127 - 7
    else:
        mant, ex = np.frexp(amax / 6.0)
        byte = np.where(mant > 0.5, ex, ex - 1) + 127
    byte = np.clip(np.where(amax > 0, byte, 1), 1, 254)
    scaled = (w * np.exp2(127.0 - byte)[:, None, :]).reshape(k, n).astype(np.float32)
    by_word = np.ascontiguousarray(scaled.reshape(k // 512, 128, 4, n).transpose(0, 1, 3, 2))
    if fmt == "e4m3":
        words = by_word.astype(ml_dtypes.float8_e4m3fn).view(np.uint8)
    else:
        c = by_word.astype(ml_dtypes.float4_e2m1fn).view(np.uint8) & 0xF
        words = (c[..., 0::2] | (c[..., 1::2] << 4)).reshape(k // 512, 128, 2 * n)
    return np.ascontiguousarray(words), np.ascontiguousarray(byte.astype(np.uint8).reshape(k // 512, 16, n))


def unpack_weight(words, scales, fmt):
    g, _, n = scales.shape
    words = np.ascontiguousarray(words).reshape(g, 128, n, -1)
    if fmt == "e4m3":
        vals = words.view(ml_dtypes.float8_e4m3fn).astype(np.float64)
    else:
        nib = np.empty((g, 128, n, 4), np.uint8)
        nib[..., 0::2] = words & 0xF
        nib[..., 1::2] = words >> 4
        vals = E2M1[nib]
    vals = vals * np.repeat(np.exp2(scales.astype(np.float64) - 127.0), 8, axis=1)[..., None]
    return vals.transpose(0, 1, 3, 2).reshape(g * 512, n)


def gelu(v):
    return 0.5 * v * (1.0 + np.tanh(np.sqrt(2.0 / np.pi) * (v + 0.044715 * v**3)))


K, R, N, T, S = 1024, 512, 1024, 2048, 1024

def setup_inputs():
    n = np.random.standard_normal
    s = mx_kscale(K)[:, None]
    u = mx_kscale(R)[:, None]
    tab_words, tab_scales = pack_weight(n((K, T)) * s, "e4m3")
    w4_words, w4_scales = pack_weight(n((K, N)) / np.sqrt(K) / s, "e2m1")
    return {
        "tab_words": tab_words,
        "tab_scales": tab_scales,
        "offs": striped(np.random.permutation(T)[:S]),
        "gT": np.exp(0.4 * n((R, T))).astype(np.float32),
        "w4_words": w4_words,
        "w4_scales": w4_scales,
        "wa": (n((K, R)) / np.sqrt(K) / s * u.T).astype(np.float32),
        "wb": (0.8 * n((R, N)) / np.sqrt(R) / u).astype(np.float32),
        "bias": (0.5 * n(N)).astype(np.float32),
    }

def reference(tab_words, tab_scales, offs, gT, w4_words, w4_scales, wa, wb, bias):
    v = unpack_weight(tab_words, tab_scales, "e4m3")[:, unstriped(offs)]
    g = f64(gT)[:, unstriped(offs)]
    w4 = unpack_weight(w4_words, w4_scales, "e2m1")
    a = mxq(f64(wa), 0, "e4m3").T @ v
    h = mxq(g * a, 0, "e4m3")
    y = w4.T @ v + mxq(f64(wb), 0, "e4m3").T @ h
    return y + f64(bias)[:, None]

@@ -1,0 +1,280 @@
+from contextlib import ExitStack
+
+import concourse.mybir as mybir
+from concourse.masks import make_identity
+
+K, R, N, T, S = 1024, 512, 1024, 2048, 1024
+FLOPS = 2 * S * (K * R + K * N + R * N)
+
+F32 = mybir.dt.float32
+BF16 = mybir.dt.bfloat16
+I32 = mybir.dt.int32
+U32 = mybir.dt.uint32
+U16 = mybir.dt.uint16
+U8 = mybir.dt.uint8
+FP8X4 = mybir.dt.float8_e4m3fn_x4
+FP4X4 = mybir.dt.float4_e2m1fn_x4
+MULT = mybir.AluOpType.mult
+ADD = mybir.AluOpType.add
+IDENTITY = mybir.ActivationFunctionType.Identity
+
+P = 128
+PACK = 4
+PASSES = K // (P * PACK)
+HALF = 512
+HALVES = S // HALF
+N_TILES = N // P
+WB_COLS = 256
+WB_CHUNKS = N // WB_COLS
+WB_EARLY = 2
+
+
+def tile_list_lora_cached_projection_kernel(
+    tc, tab_words, tab_scales, offs, gT, w4_words, w4_scales, wa, wb, bias, out
+):
+    nc = tc.nc
+    with ExitStack() as ctx:
+        keep = ctx.enter_context(tc.tile_pool(name="keep", bufs=1))
+        psum = ctx.enter_context(tc.psum_pool(name="psum", bufs=8))
+
+        def tile(name, shape, dtype, slot=None, bufs=1):
+            return keep.tile(shape, dtype, name=name, tag=slot or name, bufs=bufs, align_bytes=64)
+
+        reused = ctx.enter_context(tc.tile_pool(name="reused", bufs=1))
+
+        def placed(name, shape, dtype, offset):
+            return reused.tile(shape, dtype, name=name, offset=offset, align_bytes=64)
+
+        def bank(name):
+            return psum.tile([P, HALF], F32, name=name, tag="bank")
+
+        offsets = keep.tile([P, S // 16], U16, name="offsets")
+        nc.sync.dma_start(offsets[:], offs)
+
+        def picks(half):
+            return offsets[:, half * (HALF // 16) : (half + 1) * (HALF // 16)]
+
+        def load_scale_rows(planes, scales):
+            for q in range(4):
+                nc.sync.dma_start(
+                    out=planes[32 * q : 32 * q + 4, :, :],
+                    in_=scales[:, 4 * q : 4 * q + 4, :].rearrange("a r c -> r a c").bitcast(I32),
+                )
+
+        tab_planes = tile("tab_planes", [P, PASSES, T // 4], I32)
+        nc.vector.memset(tab_planes[:], 0)
+        w4_planes = tile("w4_planes", [P, PASSES, N // 4], I32)
+        nc.vector.memset(w4_planes[:], 0)
+        bias_rows = tile("bias_rows", [P, P], F32)
+        nc.gpsimd.memset(bias_rows[:], 0.0)
+        identity = tile("identity", [P, P], F32)
+        make_identity(nc, identity[:])
+
+        wa_raw = [tile(f"wa_raw{a}", [P, PACK, R], F32) for a in range(PASSES)]
+        tab_w = [placed("tab_w0", [P, T], I32, 0), tile("tab_w1", [P, T], I32)]
+
+        def load_words(a):
+            nc.sync.dma_start(out=tab_w[a][:], in_=tab_words[a].rearrange("p t i -> p (t i)").bitcast(I32))
+
+        def load_wa(a):
+            nc.sync.dma_start(
+                out=wa_raw[a][:],
+                in_=wa[a * P * PACK : (a + 1) * P * PACK, :].rearrange("(p j) r -> p j r", j=PACK),
+            )
+
+        load_words(0)
+        load_wa(0)
+        load_scale_rows(tab_planes, tab_scales)
+        nc.sync.dma_start(out=bias_rows[0:N_TILES, :], in_=bias.rearrange("(c p) -> c p", p=P))
+        load_wa(1)
+        load_words(1)
+        load_scale_rows(w4_planes, w4_scales)
+        w4_codes = [tile(f"w4_codes{u}", [P, PASSES, N], U8) for u in range(2)]
+
+        def load_w4(u):
+            nc.sync.dma_start(
+                out=w4_codes[u][:].bitcast(I32),
+                in_=w4_words[:, :, u * N : (u + 1) * N].rearrange("a p b -> p a b").bitcast(I32),
+            )
+
+        wb_raw = [tile(f"wb_raw{c}", [P, PACK, WB_COLS], F32) for c in range(WB_CHUNKS)]
+
+        def load_wb(c):
+            nc.sync.dma_start(
+                out=wb_raw[c][:],
+                in_=wb[:, c * WB_COLS : (c + 1) * WB_COLS].rearrange("(p j) n -> p j n", j=PACK),
+            )
+
+        g_rows = gT.rearrange("(p j) t -> j p t", j=PACK)
+        g_tab = [tile(f"g_tab{j}", [P, T], F32) for j in range(PACK)]
+        load_w4(0)
+        for c in range(WB_EARLY):
+            load_wb(c)
+        for j in range(PACK):
+            nc.sync.dma_start(out=g_tab[j][:], in_=g_rows[j])
+        load_wb(WB_EARLY)
+        load_w4(1)
+        for c in range(WB_EARLY + 1, WB_CHUNKS):
+            load_wb(c)
+
+        def copy_on(engine, dst, src):
+            if engine is nc.scalar:
+                nc.scalar.copy(dst, src)
+            else:
+                nc.vector.tensor_copy(dst, src)
+
+        def interleave(engine, grouped, raw):
+            copy_on(
+                engine,
+                grouped.rearrange("p (c i j) -> p c j i", i=4, j=PACK),
+                raw[:].rearrange("p j (c i) -> p c j i", i=4),
+            )
+            return grouped
+
+        def quantize(name, grouped, cols, codes=None):
+            if codes is None:
+                codes = tile(name + "_codes", [P, cols], U32)
+            plane = tile(name + "_plane", [P, cols], U8)
+            nc.vector.quantize_mx(out=codes[:].bitcast(FP8X4), scales=plane[:], in_=grouped)
+            return codes, plane
+
+        def tokens(half):
+            return slice(half * HALF, (half + 1) * HALF)
+
+        v_codes = {}
+
+        def gather_words(a, half, slot=None, offset=None):
+            if offset is None:
+                v_codes[a, half] = tile(f"v_codes{a}_{half}", [P, HALF], U32, slot)
+            else:
+                v_codes[a, half] = placed(f"v_codes{a}_{half}", [P, HALF], U32, offset)
+            nc.vector.tensor_copy(v_codes[a, half][:], tab_w[a][:].bitcast(U32).indirect(picks(half)))
+
+        wa_q = {}
+        wa_codes = tile("wa_codes", [P, PASSES, R], U32)
+
+        def quantize_wa(a):
+            wa_grouped = placed(f"wa_grouped{a}", [P, R * PACK], BF16, 1024 + 4096 * a)
+            nc.scalar.copy(
+                wa_grouped[:].rearrange("p (t m j) -> p m j t", t=PACK, j=PACK),
+                wa_raw[a][:].rearrange("p j (m t) -> p m j t", t=PACK),
+            )
+            wa_q[a] = quantize(f"wa{a}", wa_grouped[:], R, wa_codes[:, a, :])
+
+        gather_words(0, 0)
+        gather_words(0, 1)
+        v_plane = {}
+
+        def gather_plane(a):
+            v_plane[a] = placed(f"v_plane{a}", [P, S], U8, 1024 * a)
+            nc.vector.tensor_copy(v_plane[a][:], tab_planes[:, a, :].bitcast(U8).indirect(offsets[:]))
+
+        gather_plane(0)
+        quantize_wa(0)
+        gather_plane(1)
+        gather_words(1, 0, "tab_planes")
+        quantize_wa(1)
+        gather_words(1, 1, offset=5120)
+
+        bias_bank = bank("bias_bank")
+        nc.tensor.transpose(bias_bank[:, 0:P], bias_rows[:], identity[:])
+        bias_cols = tile("bias_cols", [P, N_TILES], F32)
+        nc.scalar.activation(bias_cols[:], bias_bank[:, 0:N_TILES], IDENTITY)
+
+        down_acc = {}
+        for j in range(PACK):
+            for half in range(HALVES):
+                acc = bank(f"down_acc{half}_{j}")
+                cols = slice(j * P, (j + 1) * P)
+                for a in range(PASSES):
+                    codes, plane = wa_q[a]
+                    nc.tensor.matmul_mx(
+                        out=acc[:],
+                        lhsT=codes[:, cols].bitcast(FP8X4),
+                        lhsT_scale=plane[:, cols],
+                        rhs=v_codes[a, half][:].bitcast(FP8X4),
+                        rhs_scale=v_plane[a][:, tokens(half)],
+                        start=(a == 0),
+                        stop=(a == PASSES - 1),
+                    )
+                down_acc[half, j] = acc
+
+        wb_q = {}
+        late_codes = []
+
+        wb_early = tile("wb_early", [P, WB_EARLY, WB_COLS * PACK], BF16)
+        wb_late = []
+
+        def quantize_wb(c):
+            grouped = wb_early[:, c, :] if c < WB_EARLY else wb_late[0][:, c - WB_EARLY, :]
+            codes = None if c < WB_EARLY else late_codes[0][:, c - WB_EARLY, :]
+            wb_q[c] = quantize(f"wb{c}", interleave(nc.scalar, grouped, wb_raw[c]), WB_COLS, codes)
+
+        for c in range(WB_EARLY):
+            quantize_wb(c)
+
+        def base_passes(half, n):
+            acc = bank(f"y_acc{half}_{n}")
+            u, c = divmod(n, N_TILES // 2)
+            for a in range(PASSES):
+                nc.tensor.matmul_mx(
+                    out=acc[:],
+                    lhsT=w4_codes[u][:, a, 2 * c * P : 2 * (c + 1) * P].bitcast(FP4X4),
+                    lhsT_scale=w4_planes[:, a, :].bitcast(U8)[:, n * P : (n + 1) * P],
+                    rhs=v_codes[a, half][:].bitcast(FP8X4),
+                    rhs_scale=v_plane[a][:, tokens(half)],
+                    start=(a == 0),
+                    stop=False,
+                )
+            return acc
+
+        h_f32 = [
+            keep.tile([P, PACK, HALF], F32, name=f"h_f32_{half}", tag=f"h_f32_{half}", align_bytes=64)
+            for half in range(HALVES)
+        ]
+
+        def scale_down(half, j, slot="down", bufs=2):
+            down = tile(f"down{half}_{j}", [P, HALF], F32, slot, bufs)
+            nc.scalar.copy(down[:], down_acc[half, j][:])
+            nc.vector.tensor_tensor(h_f32[half][:, j, :], g_tab[j][:].indirect(picks(half)), down[:], MULT)
+
+        def quantize_h(half):
+            grouped = tile(f"h_grouped{half}", [P, HALF * PACK], BF16)
+            return quantize(f"h{half}", interleave(nc.vector, grouped[:], h_f32[half]), HALF)
+
+        def finish(half, n, acc, h_q, engine):
+            c, first = divmod(n * P, WB_COLS)
+            codes, plane = wb_q[c]
+            nc.tensor.matmul_mx(
+                out=acc[:],
+                lhsT=codes[:, first : first + P].bitcast(FP8X4),
+                lhsT_scale=plane[:, first : first + P],
+                rhs=h_q[0][:].bitcast(FP8X4),
+                rhs_scale=h_q[1][:],
+                start=False,
+                stop=True,
+            )
+            result = tile(f"result{half}_{n}", [P, HALF], F32)
+            if engine is nc.scalar:
+                nc.scalar.activation(result[:], acc[:], IDENTITY, bias=bias_cols[:, n : n + 1])
+            else:
+                nc.vector.tensor_scalar(result[:], acc[:], bias_cols[:, n : n + 1], None, ADD)
+            nc.sync.dma_start(out=out[n * P : (n + 1) * P, half * HALF : (half + 1) * HALF], in_=result[:])
+
+        for j in range(PACK - 1):
+            for half in range(HALVES):
+                scale_down(half, j)
+        scale_down(0, PACK - 1)
+        h_first = quantize_h(0)
+        scale_down(1, PACK - 1, "h_f32_0", 1)
+        late_codes.append(tile("wb_late_codes", [P, WB_CHUNKS - WB_EARLY, WB_COLS], U32, "h_f32_0"))
+        wb_late.append(tile("wb_late", [P, WB_CHUNKS - WB_EARLY, WB_COLS * PACK], BF16, "g_tab2"))
+        first_accs = [base_passes(0, n) for n in range(N_TILES)]
+        tiles_per_chunk = WB_COLS // P
+        for n in range(N_TILES):
+            if n % tiles_per_chunk == 0 and n // tiles_per_chunk >= WB_EARLY:
+                quantize_wb(n // tiles_per_chunk)
+            finish(0, n, first_accs[n], h_first, nc.scalar)
+        h_second = quantize_h(1)
+        for n in range(N_TILES):
+            finish(1, n, base_passes(1, n), h_second, nc.vector if n % 2 == 0 else nc.scalar)

@@ -1,3 +1,4 @@
+import math
 from contextlib import ExitStack
 
 import concourse.mybir as mybir
@@ -17,16 +18,15 @@ FP4X4 = mybir.dt.float4_e2m1fn_x4
 MULT = mybir.AluOpType.mult
 ADD = mybir.AluOpType.add
 IDENTITY = mybir.ActivationFunctionType.Identity
+ELEMENT_BYTES = {F32: 4, I32: 4, U32: 4, BF16: 2, U8: 1}
 
 P = 128
 PACK = 4
 PASSES = K // (P * PACK)
 HALF = 512
-HALVES = S // HALF
 N_TILES = N // P
 WB_COLS = 256
 WB_CHUNKS = N // WB_COLS
-WB_EARLY = 2
 
 
 def tile_list_lora_cached_projection_kernel(
@@ -34,25 +34,31 @@ def tile_list_lora_cached_projection_kernel(
 ):
     nc = tc.nc
     with ExitStack() as ctx:
-        keep = ctx.enter_context(tc.tile_pool(name="keep", bufs=1))
+        lists = ctx.enter_context(tc.tile_pool(name="lists", bufs=1))
+        sbuf = ctx.enter_context(tc.tile_pool(name="sbuf", bufs=1))
         psum = ctx.enter_context(tc.psum_pool(name="psum", bufs=8))
 
-        def tile(name, shape, dtype, slot=None, bufs=1):
-            return keep.tile(shape, dtype, name=name, tag=slot or name, bufs=bufs, align_bytes=64)
+        place = {"end": 0}
 
-        reused = ctx.enter_context(tc.tile_pool(name="reused", bufs=1))
-
-        def placed(name, shape, dtype, offset):
-            return reused.tile(shape, dtype, name=name, offset=offset, align_bytes=64)
+        def tile(name, shape, dtype, over=None, skip=0):
+            if over is None:
+                place[name] = place["end"]
+                place["end"] += math.prod(shape[1:]) * ELEMENT_BYTES[dtype]
+            else:
+                place[name] = place[over] + skip
+            return sbuf.tile(shape, dtype, name=name, offset=place[name], align_bytes=64)
 
         def bank(name):
             return psum.tile([P, HALF], F32, name=name, tag="bank")
 
-        offsets = keep.tile([P, S // 16], U16, name="offsets")
+        offsets = lists.tile([P, S // 16], U16, name="offsets")
         nc.sync.dma_start(offsets[:], offs)
 
         def picks(half):
             return offsets[:, half * (HALF // 16) : (half + 1) * (HALF // 16)]
+
+        def tokens(half):
+            return slice(half * HALF, (half + 1) * HALF)
 
         def load_scale_rows(planes, scales):
             for q in range(4):
@@ -67,14 +73,20 @@ def tile_list_lora_cached_projection_kernel(
         nc.vector.memset(w4_planes[:], 0)
         bias_rows = tile("bias_rows", [P, P], F32)
         nc.gpsimd.memset(bias_rows[:], 0.0)
+        nc.sync.dma_start(out=bias_rows[0:N_TILES, :], in_=bias.rearrange("(c p) -> c p", p=P))
         identity = tile("identity", [P, P], F32)
         make_identity(nc, identity[:])
 
         wa_raw = [tile(f"wa_raw{a}", [P, PACK, R], F32) for a in range(PASSES)]
-        tab_w = [placed("tab_w0", [P, T], I32, 0), tile("tab_w1", [P, T], I32)]
+        tab_w = [tile(f"tab_w{a}", [P, T], I32) for a in range(PASSES)]
+        w4_codes = [tile(f"w4_codes{u}", [P, PASSES, N], U8) for u in range(2)]
+        wb_raw = [tile(f"wb_raw{c}", [P, PACK, WB_COLS], F32) for c in range(WB_CHUNKS)]
+        g_tab = [tile(f"g_tab{j}", [P, T], F32) for j in range(PACK)]
 
-        def load_words(a):
-            nc.sync.dma_start(out=tab_w[a][:], in_=tab_words[a].rearrange("p t i -> p (t i)").bitcast(I32))
+        def load_words(a, cols=slice(0, T)):
+            nc.sync.dma_start(
+                out=tab_w[a][:, cols], in_=tab_words[a].rearrange("p t i -> p (t i)").bitcast(I32)[:, cols]
+            )
 
         def load_wa(a):
             nc.sync.dma_start(
@@ -82,22 +94,11 @@ def tile_list_lora_cached_projection_kernel(
                 in_=wa[a * P * PACK : (a + 1) * P * PACK, :].rearrange("(p j) r -> p j r", j=PACK),
             )
 
-        load_words(0)
-        load_wa(0)
-        load_scale_rows(tab_planes, tab_scales)
-        nc.sync.dma_start(out=bias_rows[0:N_TILES, :], in_=bias.rearrange("(c p) -> c p", p=P))
-        load_wa(1)
-        load_words(1)
-        load_scale_rows(w4_planes, w4_scales)
-        w4_codes = [tile(f"w4_codes{u}", [P, PASSES, N], U8) for u in range(2)]
-
         def load_w4(u):
             nc.sync.dma_start(
                 out=w4_codes[u][:].bitcast(I32),
                 in_=w4_words[:, :, u * N : (u + 1) * N].rearrange("a p b -> p a b").bitcast(I32),
             )
-
-        wb_raw = [tile(f"wb_raw{c}", [P, PACK, WB_COLS], F32) for c in range(WB_CHUNKS)]
 
         def load_wb(c):
             nc.sync.dma_start(
@@ -105,88 +106,78 @@ def tile_list_lora_cached_projection_kernel(
                 in_=wb[:, c * WB_COLS : (c + 1) * WB_COLS].rearrange("(p j) n -> p j n", j=PACK),
             )
 
-        g_rows = gT.rearrange("(p j) t -> j p t", j=PACK)
-        g_tab = [tile(f"g_tab{j}", [P, T], F32) for j in range(PACK)]
+        def load_g(j):
+            nc.sync.dma_start(out=g_tab[j][:], in_=gT.rearrange("(p j) t -> j p t", j=PACK)[j])
+
+        load_words(0, slice(0, T // 2))
+        load_words(0, slice(T // 2, T))
+        load_scale_rows(tab_planes, tab_scales)
+        load_wa(0)
+        load_wa(1)
+        load_words(1)
+        load_scale_rows(w4_planes, w4_scales)
         load_w4(0)
-        for c in range(WB_EARLY):
-            load_wb(c)
-        for j in range(PACK):
-            nc.sync.dma_start(out=g_tab[j][:], in_=g_rows[j])
-        load_wb(WB_EARLY)
+        load_wb(0)
+        load_g(0)
+        load_wb(1)
+        for j in range(1, PACK):
+            load_g(j)
         load_w4(1)
-        for c in range(WB_EARLY + 1, WB_CHUNKS):
-            load_wb(c)
-
-        def copy_on(engine, dst, src):
-            if engine is nc.scalar:
-                nc.scalar.copy(dst, src)
-            else:
-                nc.vector.tensor_copy(dst, src)
-
-        def interleave(engine, grouped, raw):
-            copy_on(
-                engine,
-                grouped.rearrange("p (c i j) -> p c j i", i=4, j=PACK),
-                raw[:].rearrange("p j (c i) -> p c j i", i=4),
-            )
-            return grouped
-
-        def quantize(name, grouped, cols, codes=None):
-            if codes is None:
-                codes = tile(name + "_codes", [P, cols], U32)
-            plane = tile(name + "_plane", [P, cols], U8)
-            nc.vector.quantize_mx(out=codes[:].bitcast(FP8X4), scales=plane[:], in_=grouped)
-            return codes, plane
-
-        def tokens(half):
-            return slice(half * HALF, (half + 1) * HALF)
-
-        v_codes = {}
-
-        def gather_words(a, half, slot=None, offset=None):
-            if offset is None:
-                v_codes[a, half] = tile(f"v_codes{a}_{half}", [P, HALF], U32, slot)
-            else:
-                v_codes[a, half] = placed(f"v_codes{a}_{half}", [P, HALF], U32, offset)
-            nc.vector.tensor_copy(v_codes[a, half][:], tab_w[a][:].bitcast(U32).indirect(picks(half)))
-
-        wa_q = {}
-        wa_codes = tile("wa_codes", [P, PASSES, R], U32)
-
-        def quantize_wa(a):
-            wa_grouped = placed(f"wa_grouped{a}", [P, R * PACK], BF16, 1024 + 4096 * a)
-            nc.scalar.copy(
-                wa_grouped[:].rearrange("p (t m j) -> p m j t", t=PACK, j=PACK),
-                wa_raw[a][:].rearrange("p j (m t) -> p m j t", t=PACK),
-            )
-            wa_q[a] = quantize(f"wa{a}", wa_grouped[:], R, wa_codes[:, a, :])
-
-        gather_words(0, 0)
-        gather_words(0, 1)
-        v_plane = {}
-
-        def gather_plane(a):
-            v_plane[a] = placed(f"v_plane{a}", [P, S], U8, 1024 * a)
-            nc.vector.tensor_copy(v_plane[a][:], tab_planes[:, a, :].bitcast(U8).indirect(offsets[:]))
-
-        gather_plane(0)
-        quantize_wa(0)
-        gather_plane(1)
-        gather_words(1, 0, "tab_planes")
-        quantize_wa(1)
-        gather_words(1, 1, offset=5120)
+        load_wb(2)
+        load_wb(3)
 
         bias_bank = bank("bias_bank")
         nc.tensor.transpose(bias_bank[:, 0:P], bias_rows[:], identity[:])
-        bias_cols = tile("bias_cols", [P, N_TILES], F32)
-        nc.scalar.activation(bias_cols[:], bias_bank[:, 0:N_TILES], IDENTITY)
+        bias_cols = tile("bias_cols", [P, 2 * N_TILES], F32)
+        nc.scalar.activation(bias_cols[:, 0:N_TILES], bias_bank[:, 0:N_TILES], IDENTITY)
+
+        def interleaved_views(grouped, raw):
+            return (
+                grouped.rearrange("p (c i j) -> p c j i", i=4, j=PACK),
+                raw.rearrange("p j (c i) -> p c j i", i=4),
+            )
+
+        def quantize(name, grouped, cols, over=None, skip=0):
+            codes = tile(name + "_codes", [P, cols], U32, over, skip)
+            plane = tile(name + "_plane", [P, cols], U8)
+            nc.vector.quantize_mx(out=codes[:].bitcast(FP8X4), scales=plane[:], in_=grouped[:])
+            return codes, plane
+
+        v_codes = {}
+        v_plane = {}
+
+        def gather_words(a, half, over=None):
+            v_codes[a, half] = tile(f"v_codes{a}_{half}", [P, HALF], U32, over)
+            nc.vector.tensor_copy(v_codes[a, half][:], tab_w[a][:].bitcast(U32).indirect(picks(half)))
+
+        def gather_plane(a):
+            v_plane[a] = tile(f"v_plane{a}", [P, S], U8, "tab_w0", a * S)
+            nc.vector.tensor_copy(v_plane[a][:], tab_planes[:, a, :].bitcast(U8).indirect(offsets[:]))
+
+        def round_wa(a, over=None):
+            grouped = tile(f"wa_grouped{a}", [P, R * PACK], BF16, over)
+            nc.scalar.copy(
+                grouped[:].rearrange("p (t m j) -> p m j t", t=PACK, j=PACK),
+                wa_raw[a][:].rearrange("p j (m t) -> p m j t", t=PACK),
+            )
+            return grouped
+
+        gather_words(0, 0)
+        gather_words(0, 1)
+        gather_plane(0)
+        gather_plane(1)
+        wa_q = [quantize("wa0", round_wa(0), R, "tab_planes")]
+        gather_words(1, 0, "wa_grouped0")
+        wa_q.append(quantize("wa1", round_wa(1, "wa_raw0"), R, "wa_grouped0", HALF * 4))
+        gather_words(1, 1, "wa_grouped1")
 
         down_acc = {}
         for j in range(PACK):
-            for half in range(HALVES):
+            for half in range(2):
                 acc = bank(f"down_acc{half}_{j}")
                 cols = slice(j * P, (j + 1) * P)
-                for a in range(PASSES):
+                order = (0, 1) if half == 0 else (1, 0)
+                for a in order:
                     codes, plane = wa_q[a]
                     nc.tensor.matmul_mx(
                         out=acc[:],
@@ -194,24 +185,17 @@ def tile_list_lora_cached_projection_kernel(
                         lhsT_scale=plane[:, cols],
                         rhs=v_codes[a, half][:].bitcast(FP8X4),
                         rhs_scale=v_plane[a][:, tokens(half)],
-                        start=(a == 0),
-                        stop=(a == PASSES - 1),
+                        start=(a == order[0]),
+                        stop=(a == order[-1]),
                     )
                 down_acc[half, j] = acc
 
         wb_q = {}
-        late_codes = []
 
-        wb_early = tile("wb_early", [P, WB_EARLY, WB_COLS * PACK], BF16)
-        wb_late = []
-
-        def quantize_wb(c):
-            grouped = wb_early[:, c, :] if c < WB_EARLY else wb_late[0][:, c - WB_EARLY, :]
-            codes = None if c < WB_EARLY else late_codes[0][:, c - WB_EARLY, :]
-            wb_q[c] = quantize(f"wb{c}", interleave(nc.scalar, grouped, wb_raw[c]), WB_COLS, codes)
-
-        for c in range(WB_EARLY):
-            quantize_wb(c)
+        def quantize_wb(c, grouped_over, codes_over=None, skip=0):
+            grouped = tile(f"wb_grouped{c}", [P, WB_COLS * PACK], BF16, grouped_over)
+            nc.scalar.copy(*interleaved_views(grouped[:], wb_raw[c][:]))
+            wb_q[c] = quantize(f"wb{c}", grouped, WB_COLS, codes_over, skip)
 
         def base_passes(half, n):
             acc = bank(f"y_acc{half}_{n}")
@@ -228,21 +212,22 @@ def tile_list_lora_cached_projection_kernel(
                 )
             return acc
 
-        h_f32 = [
-            keep.tile([P, PACK, HALF], F32, name=f"h_f32_{half}", tag=f"h_f32_{half}", align_bytes=64)
-            for half in range(HALVES)
-        ]
+        h_f32 = [tile(f"h_f32_{half}", [P, PACK, HALF], F32) for half in range(2)]
 
-        def scale_down(half, j, slot="down", bufs=2):
-            down = tile(f"down{half}_{j}", [P, HALF], F32, slot, bufs)
+        def scale_down(half, j, over):
+            down = tile(f"down{half}_{j}", [P, HALF], F32, over)
             nc.scalar.copy(down[:], down_acc[half, j][:])
             nc.vector.tensor_tensor(h_f32[half][:, j, :], g_tab[j][:].indirect(picks(half)), down[:], MULT)
 
-        def quantize_h(half):
+        def quantize_h(half, scalar_tokens):
             grouped = tile(f"h_grouped{half}", [P, HALF * PACK], BF16)
-            return quantize(f"h{half}", interleave(nc.vector, grouped[:], h_f32[half]), HALF)
+            cut = scalar_tokens * PACK
+            if scalar_tokens:
+                nc.scalar.copy(*interleaved_views(grouped[:, :cut], h_f32[half][:, :, :scalar_tokens]))
+            nc.vector.tensor_copy(*interleaved_views(grouped[:, cut:], h_f32[half][:, :, scalar_tokens:]))
+            return quantize(f"h{half}", grouped, HALF)
 
-        def finish(half, n, acc, h_q, engine):
+        def finish(half, n, acc, h_q, on_scalar):
             c, first = divmod(n * P, WB_COLS)
             codes, plane = wb_q[c]
             nc.tensor.matmul_mx(
@@ -255,26 +240,26 @@ def tile_list_lora_cached_projection_kernel(
                 stop=True,
             )
             result = tile(f"result{half}_{n}", [P, HALF], F32)
-            if engine is nc.scalar:
+            if on_scalar:
                 nc.scalar.activation(result[:], acc[:], IDENTITY, bias=bias_cols[:, n : n + 1])
             else:
                 nc.vector.tensor_scalar(result[:], acc[:], bias_cols[:, n : n + 1], None, ADD)
-            nc.sync.dma_start(out=out[n * P : (n + 1) * P, half * HALF : (half + 1) * HALF], in_=result[:])
+            nc.sync.dma_start(out=out[n * P : (n + 1) * P, tokens(half)], in_=result[:])
 
-        for j in range(PACK - 1):
-            for half in range(HALVES):
-                scale_down(half, j)
-        scale_down(0, PACK - 1)
-        h_first = quantize_h(0)
-        scale_down(1, PACK - 1, "h_f32_0", 1)
-        late_codes.append(tile("wb_late_codes", [P, WB_CHUNKS - WB_EARLY, WB_COLS], U32, "h_f32_0"))
-        wb_late.append(tile("wb_late", [P, WB_CHUNKS - WB_EARLY, WB_COLS * PACK], BF16, "g_tab2"))
+        quantize_wb(0, "wa_raw1")
+        for j in range(PACK):
+            for half in range(2):
+                scale_down(half, j, f"down{half}_{j - 1}" if j else None)
+            if j == 0:
+                quantize_wb(1, "g_tab0")
+        h_first = quantize_h(0, HALF // 2)
         first_accs = [base_passes(0, n) for n in range(N_TILES)]
-        tiles_per_chunk = WB_COLS // P
+        h_second = quantize_h(1, 0)
         for n in range(N_TILES):
-            if n % tiles_per_chunk == 0 and n // tiles_per_chunk >= WB_EARLY:
-                quantize_wb(n // tiles_per_chunk)
-            finish(0, n, first_accs[n], h_first, nc.scalar)
-        h_second = quantize_h(1)
+            if n == 0:
+                quantize_wb(2, "g_tab3")
+            if n == 2:
+                quantize_wb(3, "wb_grouped2")
+            finish(0, n, first_accs[n], h_first, n < 6)
         for n in range(N_TILES):
-            finish(1, n, base_passes(1, n), h_second, nc.vector if n % 2 == 0 else nc.scalar)
+            finish(1, n, base_passes(1, n), h_second, n % 2 == 0)

@@ -36,7 +36,7 @@ def tile_list_lora_cached_projection_kernel(
     with ExitStack() as ctx:
         lists = ctx.enter_context(tc.tile_pool(name="lists", bufs=1))
         sbuf = ctx.enter_context(tc.tile_pool(name="sbuf", bufs=1))
-        psum = ctx.enter_context(tc.psum_pool(name="psum", bufs=8))
+        psum = ctx.enter_context(tc.psum_pool(name="psum", bufs=1))
 
         place = {"end": 0}
 
@@ -48,8 +48,8 @@ def tile_list_lora_cached_projection_kernel(
                 place[name] = place[over] + skip
             return sbuf.tile(shape, dtype, name=name, offset=place[name], align_bytes=64)
 
-        def bank(name):
-            return psum.tile([P, HALF], F32, name=name, tag="bank")
+        def bank(name, number):
+            return psum.tile([P, HALF], F32, name=name, tag=f"bank{number}")
 
         offsets = lists.tile([P, S // 16], U16, name="offsets")
         nc.sync.dma_start(offsets[:], offs)
@@ -126,7 +126,7 @@ def tile_list_lora_cached_projection_kernel(
         load_wb(2)
         load_wb(3)
 
-        bias_bank = bank("bias_bank")
+        bias_bank = bank("bias_bank", N_TILES - 1)
         nc.tensor.transpose(bias_bank[:, 0:P], bias_rows[:], identity[:])
         bias_cols = tile("bias_cols", [P, 2 * N_TILES], F32)
         nc.scalar.activation(bias_cols[:, 0:N_TILES], bias_bank[:, 0:N_TILES], IDENTITY)
@@ -174,7 +174,7 @@ def tile_list_lora_cached_projection_kernel(
         down_acc = {}
         for j in range(PACK):
             for half in range(2):
-                acc = bank(f"down_acc{half}_{j}")
+                acc = bank(f"down_acc{half}_{j}", 2 * j + half)
                 cols = slice(j * P, (j + 1) * P)
                 order = (0, 1) if half == 0 else (1, 0)
                 for a in order:
@@ -192,13 +192,13 @@ def tile_list_lora_cached_projection_kernel(
 
         wb_q = {}
 
-        def quantize_wb(c, grouped_over, codes_over=None, skip=0):
-            grouped = tile(f"wb_grouped{c}", [P, WB_COLS * PACK], BF16, grouped_over)
-            nc.scalar.copy(*interleaved_views(grouped[:], wb_raw[c][:]))
-            wb_q[c] = quantize(f"wb{c}", grouped, WB_COLS, codes_over, skip)
+        def quantize_wb(c, over, copy=nc.scalar.copy):
+            grouped = tile(f"wb_grouped{c}", [P, WB_COLS * PACK], BF16, over)
+            copy(*interleaved_views(grouped[:], wb_raw[c][:]))
+            wb_q[c] = quantize(f"wb{c}", grouped, WB_COLS)
 
         def base_passes(half, n):
-            acc = bank(f"y_acc{half}_{n}")
+            acc = bank(f"y_acc{half}_{n}", n)
             u, c = divmod(n, N_TILES // 2)
             for a in range(PASSES):
                 nc.tensor.matmul_mx(
@@ -219,8 +219,8 @@ def tile_list_lora_cached_projection_kernel(
             nc.scalar.copy(down[:], down_acc[half, j][:])
             nc.vector.tensor_tensor(h_f32[half][:, j, :], g_tab[j][:].indirect(picks(half)), down[:], MULT)
 
-        def quantize_h(half, scalar_tokens):
-            grouped = tile(f"h_grouped{half}", [P, HALF * PACK], BF16)
+        def quantize_h(half, scalar_tokens, over=None):
+            grouped = tile(f"h_grouped{half}", [P, HALF * PACK], BF16, over)
             cut = scalar_tokens * PACK
             if scalar_tokens:
                 nc.scalar.copy(*interleaved_views(grouped[:, :cut], h_f32[half][:, :, :scalar_tokens]))
@@ -254,12 +254,10 @@ def tile_list_lora_cached_projection_kernel(
                 quantize_wb(1, "g_tab0")
         h_first = quantize_h(0, HALF // 2)
         first_accs = [base_passes(0, n) for n in range(N_TILES)]
-        h_second = quantize_h(1, 0)
+        quantize_wb(2, "h_f32_0")
+        h_second = quantize_h(1, 0, "h_grouped0")
+        quantize_wb(3, "h_grouped1", nc.vector.tensor_copy)
         for n in range(N_TILES):
-            if n == 0:
-                quantize_wb(2, "g_tab3")
-            if n == 2:
-                quantize_wb(3, "wb_grouped2")
-            finish(0, n, first_accs[n], h_first, n < 6)
+            finish(0, n, first_accs[n], h_first, True)
         for n in range(N_TILES):
-            finish(1, n, base_passes(1, n), h_second, n % 2 == 0)
+            finish(1, n, base_passes(1, n), h_second, n % 2 == 1)

@@ -26,7 +26,6 @@ PASSES = K // (P * PACK)
 HALF = 512
 N_TILES = N // P
 WB_COLS = 256
-WB_CHUNKS = N // WB_COLS
 
 
 def tile_list_lora_cached_projection_kernel(
@@ -52,7 +51,6 @@ def tile_list_lora_cached_projection_kernel(
             return psum.tile([P, HALF], F32, name=name, tag=f"bank{number}")
 
         offsets = lists.tile([P, S // 16], U16, name="offsets")
-        nc.sync.dma_start(offsets[:], offs)
 
         def picks(half):
             return offsets[:, half * (HALF // 16) : (half + 1) * (HALF // 16)]
@@ -60,33 +58,7 @@ def tile_list_lora_cached_projection_kernel(
         def tokens(half):
             return slice(half * HALF, (half + 1) * HALF)
 
-        def load_scale_rows(planes, scales):
-            for q in range(4):
-                nc.sync.dma_start(
-                    out=planes[32 * q : 32 * q + 4, :, :],
-                    in_=scales[:, 4 * q : 4 * q + 4, :].rearrange("a r c -> r a c").bitcast(I32),
-                )
-
-        tab_planes = tile("tab_planes", [P, PASSES, T // 4], I32)
-        nc.vector.memset(tab_planes[:], 0)
-        w4_planes = tile("w4_planes", [P, PASSES, N // 4], I32)
-        nc.vector.memset(w4_planes[:], 0)
-        bias_rows = tile("bias_rows", [P, P], F32)
-        nc.gpsimd.memset(bias_rows[:], 0.0)
-        nc.sync.dma_start(out=bias_rows[0:N_TILES, :], in_=bias.rearrange("(c p) -> c p", p=P))
-        identity = tile("identity", [P, P], F32)
-        make_identity(nc, identity[:])
-
         wa_raw = [tile(f"wa_raw{a}", [P, PACK, R], F32) for a in range(PASSES)]
-        tab_w = [tile(f"tab_w{a}", [P, T], I32) for a in range(PASSES)]
-        w4_codes = [tile(f"w4_codes{u}", [P, PASSES, N], U8) for u in range(2)]
-        wb_raw = [tile(f"wb_raw{c}", [P, PACK, WB_COLS], F32) for c in range(WB_CHUNKS)]
-        g_tab = [tile(f"g_tab{j}", [P, T], F32) for j in range(PACK)]
-
-        def load_words(a, cols=slice(0, T)):
-            nc.sync.dma_start(
-                out=tab_w[a][:, cols], in_=tab_words[a].rearrange("p t i -> p (t i)").bitcast(I32)[:, cols]
-            )
 
         def load_wa(a):
             nc.sync.dma_start(
@@ -94,42 +66,76 @@ def tile_list_lora_cached_projection_kernel(
                 in_=wa[a * P * PACK : (a + 1) * P * PACK, :].rearrange("(p j) r -> p j r", j=PACK),
             )
 
+        scale_rows = tile("scale_rows", [P, T // 4], I32)
+        for q in range(4):
+            nc.sync.dma_start(
+                out=scale_rows[32 * q : 32 * q + 8, :], in_=tab_scales[:, 4 * q : 4 * q + 4, :].bitcast(I32)
+            )
+        nc.sync.dma_start(offsets[:], offs)
+        bias_rows = tile("bias_rows", [P, P], F32)
+        nc.gpsimd.memset(bias_rows[:], 0.0)
+        nc.sync.dma_start(out=bias_rows[0:N_TILES, :], in_=bias.rearrange("(c p) -> c p", p=P))
+        tab_planes = tile("tab_planes", [P, T // 4], I32)
+        nc.vector.memset(tab_planes[:], 0)
+        w4_planes = tile("w4_planes", [P, PASSES, N // 4], I32)
+        nc.vector.memset(w4_planes[:], 0)
+        moved_plane = tile("moved_plane", [P, S // 4], I32)
+        nc.vector.memset(moved_plane[:], 0)
+        for q in range(4):
+            nc.vector.tensor_copy(tab_planes[32 * q : 32 * q + 8, :], scale_rows[32 * q : 32 * q + 8, :])
+        identity = tile("identity", [P, P], F32)
+        make_identity(nc, identity[:])
+
+        tab_w = [tile(f"tab_w{a}", [P, T], I32) for a in range(PASSES)]
+        w4_codes = [tile(f"w4_codes{u}", [P, PASSES, N], U8) for u in range(2)]
+        g_tab = [tile(f"g_tab{j}", [P, T], F32) for j in range(PACK)]
+        wb_raw = {}
+
+        def load_words(a):
+            nc.sync.dma_start(out=tab_w[a][:], in_=tab_words[a].rearrange("p t i -> p (t i)").bitcast(I32))
+
         def load_w4(u):
             nc.sync.dma_start(
                 out=w4_codes[u][:].bitcast(I32),
                 in_=w4_words[:, :, u * N : (u + 1) * N].rearrange("a p b -> p a b").bitcast(I32),
             )
 
-        def load_wb(c):
+        def load_wb(first, count):
+            raw = tile(f"wb_raw{first}", [P, PACK, count * WB_COLS], F32)
             nc.sync.dma_start(
-                out=wb_raw[c][:],
-                in_=wb[:, c * WB_COLS : (c + 1) * WB_COLS].rearrange("(p j) n -> p j n", j=PACK),
+                out=raw[:],
+                in_=wb[:, first * WB_COLS : (first + count) * WB_COLS].rearrange("(p j) n -> p j n", j=PACK),
             )
+            for c in range(count):
+                wb_raw[first + c] = raw[:, :, c * WB_COLS : (c + 1) * WB_COLS]
 
         def load_g(j):
             nc.sync.dma_start(out=g_tab[j][:], in_=gT.rearrange("(p j) t -> j p t", j=PACK)[j])
 
-        load_words(0, slice(0, T // 2))
-        load_words(0, slice(T // 2, T))
-        load_scale_rows(tab_planes, tab_scales)
         load_wa(0)
+        load_words(0)
         load_wa(1)
         load_words(1)
-        load_scale_rows(w4_planes, w4_scales)
-        load_w4(0)
-        load_wb(0)
-        load_g(0)
-        load_wb(1)
-        for j in range(1, PACK):
-            load_g(j)
-        load_w4(1)
-        load_wb(2)
-        load_wb(3)
 
-        bias_bank = bank("bias_bank", N_TILES - 1)
-        nc.tensor.transpose(bias_bank[:, 0:P], bias_rows[:], identity[:])
-        bias_cols = tile("bias_cols", [P, 2 * N_TILES], F32)
-        nc.scalar.activation(bias_cols[:, 0:N_TILES], bias_bank[:, 0:N_TILES], IDENTITY)
+        v_plane = tile("v_plane", [P, S], U8)
+        nc.vector.tensor_copy(v_plane[:], tab_planes[:].bitcast(U8).indirect(offsets[:]))
+
+        load_g(0)
+        for r in range(4):
+            nc.sync.dma_start(
+                out=w4_planes[r:P:32, :, :],
+                in_=w4_scales[:, r:16:4, :].rearrange("a q c -> q a c").bitcast(I32),
+            )
+        load_g(1)
+        load_w4(0)
+        load_g(2)
+        for r in range(4):
+            nc.sync.dma_start(out=moved_plane[r:P:32, :], in_=v_plane[4 + r : P : 32, :].bitcast(I32))
+        load_g(3)
+        load_wb(0, 1)
+        load_wb(1, 1)
+        load_w4(1)
+        load_wb(2, 2)
 
         def interleaved_views(grouped, raw):
             return (
@@ -144,15 +150,10 @@ def tile_list_lora_cached_projection_kernel(
             return codes, plane
 
         v_codes = {}
-        v_plane = {}
 
-        def gather_words(a, half, over=None):
-            v_codes[a, half] = tile(f"v_codes{a}_{half}", [P, HALF], U32, over)
+        def gather_words(a, half, over):
+            v_codes[a, half] = tile(f"v_codes{a}_{half}", [P, HALF], U32, over, half * HALF * 4)
             nc.vector.tensor_copy(v_codes[a, half][:], tab_w[a][:].bitcast(U32).indirect(picks(half)))
-
-        def gather_plane(a):
-            v_plane[a] = tile(f"v_plane{a}", [P, S], U8, "tab_w0", a * S)
-            nc.vector.tensor_copy(v_plane[a][:], tab_planes[:, a, :].bitcast(U8).indirect(offsets[:]))
 
         def round_wa(a, over=None):
             grouped = tile(f"wa_grouped{a}", [P, R * PACK], BF16, over)
@@ -162,80 +163,103 @@ def tile_list_lora_cached_projection_kernel(
             )
             return grouped
 
-        gather_words(0, 0)
-        gather_words(0, 1)
-        gather_plane(0)
-        gather_plane(1)
-        wa_q = [quantize("wa0", round_wa(0), R, "tab_planes")]
-        gather_words(1, 0, "wa_grouped0")
-        wa_q.append(quantize("wa1", round_wa(1, "wa_raw0"), R, "wa_grouped0", HALF * 4))
-        gather_words(1, 1, "wa_grouped1")
+        wa_grouped = [round_wa(0)]
+        bias_bank = bank("bias_bank", N_TILES - 1)
+        nc.tensor.transpose(bias_bank[:, 0:P], bias_rows[:], identity[:])
+        bias_cols = tile("bias_cols", [P, 2 * N_TILES], F32)
+        nc.scalar.activation(bias_cols[:, 0:N_TILES], bias_bank[:, 0:N_TILES], IDENTITY)
+        wa_grouped.append(round_wa(1))
 
-        down_acc = {}
-        for j in range(PACK):
-            for half in range(2):
-                acc = bank(f"down_acc{half}_{j}", 2 * j + half)
-                cols = slice(j * P, (j + 1) * P)
-                order = (0, 1) if half == 0 else (1, 0)
-                for a in order:
-                    codes, plane = wa_q[a]
-                    nc.tensor.matmul_mx(
-                        out=acc[:],
-                        lhsT=codes[:, cols].bitcast(FP8X4),
-                        lhsT_scale=plane[:, cols],
-                        rhs=v_codes[a, half][:].bitcast(FP8X4),
-                        rhs_scale=v_plane[a][:, tokens(half)],
-                        start=(a == order[0]),
-                        stop=(a == order[-1]),
-                    )
-                down_acc[half, j] = acc
+        gather_words(0, 0, "tab_planes")
+        wa_q = [quantize("wa0", wa_grouped[0], R)]
+        gather_words(0, 1, "wa_grouped0")
+        gather_words(1, 0, "tab_w0")
+        wa_q.append(quantize("wa1", wa_grouped[1], R))
+        gather_words(1, 1, "tab_w0")
+
+        down_order = [(0, 0), (1, 0), (1, 1), (0, 1), (1, 2), (1, 3), (0, 2), (0, 3)]
+        down_acc = {key: bank(f"down_acc{key[0]}_{key[1]}", i) for i, key in enumerate(down_order)}
+
+        def down_pass(half, j, a):
+            codes, plane = wa_q[a]
+            cols = slice(j * P, (j + 1) * P)
+            nc.tensor.matmul_mx(
+                out=down_acc[half, j][:],
+                lhsT=codes[:, cols].bitcast(FP8X4),
+                lhsT_scale=plane[:, cols],
+                rhs=v_codes[a, half][:].bitcast(FP8X4),
+                rhs_scale=v_plane[4 * a : P, tokens(half)],
+                start=(a == 0),
+                stop=(a == PASSES - 1),
+            )
+
+        for half in range(2):
+            for j in range(PACK):
+                down_pass(half, j, 0)
+        for half, j in down_order:
+            down_pass(half, j, 1)
 
         wb_q = {}
+        wb_grouped = {}
 
-        def quantize_wb(c, over, copy=nc.scalar.copy):
-            grouped = tile(f"wb_grouped{c}", [P, WB_COLS * PACK], BF16, over)
-            copy(*interleaved_views(grouped[:], wb_raw[c][:]))
-            wb_q[c] = quantize(f"wb{c}", grouped, WB_COLS)
+        def round_wb(c, over, copy):
+            wb_grouped[c] = tile(f"wb_grouped{c}", [P, WB_COLS * PACK], BF16, over)
+            copy(*interleaved_views(wb_grouped[c][:], wb_raw[c]))
 
-        def base_passes(half, n):
-            acc = bank(f"y_acc{half}_{n}", n)
+        def quantize_wb(c, over=None, skip=0):
+            wb_q[c] = quantize(f"wb{c}", wb_grouped[c], WB_COLS, over, skip)
+
+        y_acc = {}
+
+        def base_pass(half, n, a):
             u, c = divmod(n, N_TILES // 2)
+            scales = v_plane[:] if a == 0 else moved_plane[:].bitcast(U8)
+            nc.tensor.matmul_mx(
+                out=y_acc[half, n][:],
+                lhsT=w4_codes[u][:, a, 2 * c * P : 2 * (c + 1) * P].bitcast(FP4X4),
+                lhsT_scale=w4_planes[:, a, :].bitcast(U8)[:, n * P : (n + 1) * P],
+                rhs=v_codes[a, half][:].bitcast(FP8X4),
+                rhs_scale=scales[:, tokens(half)],
+                start=(a == 0),
+                stop=False,
+            )
+
+        def base_passes(half, n, number):
+            y_acc[half, n] = bank(f"y_acc{half}_{n}", number)
             for a in range(PASSES):
-                nc.tensor.matmul_mx(
-                    out=acc[:],
-                    lhsT=w4_codes[u][:, a, 2 * c * P : 2 * (c + 1) * P].bitcast(FP4X4),
-                    lhsT_scale=w4_planes[:, a, :].bitcast(U8)[:, n * P : (n + 1) * P],
-                    rhs=v_codes[a, half][:].bitcast(FP8X4),
-                    rhs_scale=v_plane[a][:, tokens(half)],
-                    start=(a == 0),
-                    stop=False,
-                )
-            return acc
+                base_pass(half, n, a)
 
-        h_f32 = [tile(f"h_f32_{half}", [P, PACK, HALF], F32) for half in range(2)]
+        h_f32 = {key: tile(f"h_f32_{key[0]}_{key[1]}", [P, 2, HALF], F32) for key in [(0, 0), (0, 1), (1, 0)]}
+        down = {}
 
-        def scale_down(half, j, over):
-            down = tile(f"down{half}_{j}", [P, HALF], F32, over)
-            nc.scalar.copy(down[:], down_acc[half, j][:])
-            nc.vector.tensor_tensor(h_f32[half][:, j, :], g_tab[j][:].indirect(picks(half)), down[:], MULT)
+        def copy_down(half, j, over=None):
+            down[half, j] = tile(f"down{half}_{j}", [P, HALF], F32, over)
+            nc.scalar.copy(down[half, j][:], down_acc[half, j][:])
 
-        def quantize_h(half, scalar_tokens, over=None):
-            grouped = tile(f"h_grouped{half}", [P, HALF * PACK], BF16, over)
-            cut = scalar_tokens * PACK
-            if scalar_tokens:
-                nc.scalar.copy(*interleaved_views(grouped[:, :cut], h_f32[half][:, :, :scalar_tokens]))
-            nc.vector.tensor_copy(*interleaved_views(grouped[:, cut:], h_f32[half][:, :, scalar_tokens:]))
-            return quantize(f"h{half}", grouped, HALF)
+        def scale_down(half, j):
+            nc.vector.tensor_tensor(h_f32[half, j // 2][:, j % 2, :], g_tab[j][:].indirect(picks(half)), down[half, j][:], MULT)
 
-        def finish(half, n, acc, h_q, on_scalar):
+        h_q = {}
+
+        h_grouped = [tile(f"h_grouped{half}", [P, HALF * PACK], BF16, None) for half in range(2)]
+
+        def round_h(half, pair, copy):
+            grouped, raw = interleaved_views(h_grouped[half][:], h_f32[half, pair][:])
+            copy(grouped[:, :, 2 * pair : 2 * pair + 2, :], raw)
+
+        def quantize_h(half):
+            h_q[half] = quantize(f"h{half}", h_grouped[half], HALF)
+
+        def finish(half, n, on_scalar):
             c, first = divmod(n * P, WB_COLS)
             codes, plane = wb_q[c]
+            acc = y_acc[half, n]
             nc.tensor.matmul_mx(
                 out=acc[:],
                 lhsT=codes[:, first : first + P].bitcast(FP8X4),
                 lhsT_scale=plane[:, first : first + P],
-                rhs=h_q[0][:].bitcast(FP8X4),
-                rhs_scale=h_q[1][:],
+                rhs=h_q[half][0][:].bitcast(FP8X4),
+                rhs_scale=h_q[half][1][:],
                 start=False,
                 stop=True,
             )
@@ -246,18 +270,52 @@ def tile_list_lora_cached_projection_kernel(
                 nc.vector.tensor_scalar(result[:], acc[:], bias_cols[:, n : n + 1], None, ADD)
             nc.sync.dma_start(out=out[n * P : (n + 1) * P, tokens(half)], in_=result[:])
 
-        quantize_wb(0, "wa_raw1")
-        for j in range(PACK):
-            for half in range(2):
-                scale_down(half, j, f"down{half}_{j - 1}" if j else None)
-            if j == 0:
-                quantize_wb(1, "g_tab0")
-        h_first = quantize_h(0, HALF // 2)
-        first_accs = [base_passes(0, n) for n in range(N_TILES)]
-        quantize_wb(2, "h_f32_0")
-        h_second = quantize_h(1, 0, "h_grouped0")
-        quantize_wb(3, "h_grouped1", nc.vector.tensor_copy)
-        for n in range(N_TILES):
-            finish(0, n, first_accs[n], h_first, True)
-        for n in range(N_TILES):
-            finish(1, n, base_passes(1, n), h_second, n % 2 == 1)
+        for half, j in down_order[:6]:
+            copy_down(half, j)
+        scale_down(0, 0)
+        scale_down(1, 0)
+        copy_down(0, 2, "down1_0")
+        scale_down(0, 1)
+        round_h(0, 0, nc.scalar.copy)
+        scale_down(1, 1)
+        copy_down(0, 3, "down1_1")
+        round_h(1, 0, nc.scalar.copy)
+        scale_down(0, 2)
+        round_wb(0, "down0_2", nc.scalar.copy)
+        scale_down(0, 3)
+        for a in range(PASSES):
+            for i in range(8):
+                if a == 0:
+                    y_acc[i // 4, i % 4] = bank(f"y_acc{i // 4}_{i % 4}", i)
+                base_pass(i // 4, i % 4, a)
+        round_wb(1, "down0_3", nc.scalar.copy)
+        round_h(0, 1, nc.vector.tensor_copy)
+        quantize_wb(0)
+        quantize_h(0)
+        quantize_wb(1)
+        h_f32[1, 1] = tile("h_f32_1_1", [P, 2, HALF], F32, "down1_1")
+        scale_down(1, 2)
+        wb_grouped[2] = h_f32[1, 1][:, 1, :].bitcast(BF16)
+        nc.vector.tensor_copy(*interleaved_views(wb_grouped[2], wb_raw[2]))
+        quantize_wb(2)
+        scale_down(1, 3)
+        for n in range(4):
+            finish(0, n, True)
+        for n in range(4, 8):
+            base_passes(0, n, n - 4)
+        round_wb(3, "down1_2", nc.scalar.copy)
+        finish(0, 4, True)
+        finish(0, 5, True)
+        quantize_wb(3)
+        round_h(1, 1, nc.vector.tensor_copy)
+        quantize_h(1)
+        base_passes(1, 4, 0)
+        finish(0, 6, True)
+        finish(0, 7, True)
+        base_passes(1, 5, 1)
+        for n in range(4):
+            finish(1, n, n % 2 == 1)
+        base_passes(1, 6, 2)
+        base_passes(1, 7, 3)
+        for n in range(4, 8):
+            finish(1, n, n % 2 == 1)

@@ -26,6 +26,7 @@ PASSES = K // (P * PACK)
 HALF = 512
 N_TILES = N // P
 WB_COLS = 256
+WA_SPLIT = 48
 
 
 def tile_list_lora_cached_projection_kernel(
@@ -87,7 +88,8 @@ def tile_list_lora_cached_projection_kernel(
         make_identity(nc, identity[:])
 
         tab_w = [tile(f"tab_w{a}", [P, T], I32) for a in range(PASSES)]
-        w4_codes = [tile(f"w4_codes{u}", [P, PASSES, N], U8) for u in range(2)]
+        w4_tiles = [tile(f"w4_codes{u}", [P, (2 * PASSES * N // 2) + 2 * P], U8) for u in range(2)]
+        w4_codes = [t[:, 2 * P :].rearrange("p (a b) -> p a b", a=PASSES) for t in w4_tiles]
         g_tab = [tile(f"g_tab{j}", [P, T], F32) for j in range(PACK)]
         wb_raw = {}
 
@@ -96,14 +98,14 @@ def tile_list_lora_cached_projection_kernel(
 
         def load_w4(u):
             nc.sync.dma_start(
-                out=w4_codes[u][:].bitcast(I32),
+                out=w4_codes[u].bitcast(I32),
                 in_=w4_words[:, :, u * N : (u + 1) * N].rearrange("a p b -> p a b").bitcast(I32),
             )
 
-        def load_wb(first, count):
-            raw = tile(f"wb_raw{first}", [P, PACK, count * WB_COLS], F32)
+        def load_wb(first, count, spare=0):
+            raw = tile(f"wb_raw{first}", [P, PACK + spare, count * WB_COLS], F32)[:, 0:PACK, :]
             nc.sync.dma_start(
-                out=raw[:],
+                out=raw,
                 in_=wb[:, first * WB_COLS : (first + count) * WB_COLS].rearrange("(p j) n -> p j n", j=PACK),
             )
             for c in range(count):
@@ -112,8 +114,8 @@ def tile_list_lora_cached_projection_kernel(
         def load_g(j):
             nc.sync.dma_start(out=g_tab[j][:], in_=gT.rearrange("(p j) t -> j p t", j=PACK)[j])
 
-        load_wa(0)
         load_words(0)
+        load_wa(0)
         load_wa(1)
         load_words(1)
 
@@ -129,13 +131,14 @@ def tile_list_lora_cached_projection_kernel(
         load_g(1)
         load_w4(0)
         load_g(2)
+        load_g(3)
         for r in range(4):
             nc.sync.dma_start(out=moved_plane[r:P:32, :], in_=v_plane[4 + r : P : 32, :].bitcast(I32))
-        load_g(3)
         load_wb(0, 1)
         load_wb(1, 1)
+        load_wb(2, 1)
+        load_wb(3, 1)
         load_w4(1)
-        load_wb(2, 2)
 
         def interleaved_views(grouped, raw):
             return (
@@ -143,41 +146,44 @@ def tile_list_lora_cached_projection_kernel(
                 raw.rearrange("p j (c i) -> p c j i", i=4),
             )
 
-        def quantize(name, grouped, cols, over=None, skip=0):
+        def quantize(name, grouped, cols, over=None, skip=0, plane=None):
             codes = tile(name + "_codes", [P, cols], U32, over, skip)
-            plane = tile(name + "_plane", [P, cols], U8)
+            if plane is None:
+                plane = tile(name + "_plane", [P, cols], U8)
             nc.vector.quantize_mx(out=codes[:].bitcast(FP8X4), scales=plane[:], in_=grouped[:])
             return codes, plane
 
         v_codes = {}
 
-        def gather_words(a, half, over):
-            v_codes[a, half] = tile(f"v_codes{a}_{half}", [P, HALF], U32, over, half * HALF * 4)
+        def gather_words(a, half, over, skip=0):
+            v_codes[a, half] = tile(f"v_codes{a}_{half}", [P, HALF], U32, over, half * HALF * 4 + skip)
             nc.vector.tensor_copy(v_codes[a, half][:], tab_w[a][:].bitcast(U32).indirect(picks(half)))
 
-        def round_wa(a, over=None):
-            grouped = tile(f"wa_grouped{a}", [P, R * PACK], BF16, over)
-            nc.scalar.copy(
-                grouped[:].rearrange("p (t m j) -> p m j t", t=PACK, j=PACK),
-                wa_raw[a][:].rearrange("p j (m t) -> p m j t", t=PACK),
-            )
-            return grouped
+        wa_grouped = [tile(f"wa_grouped{a}", [P, R * PACK], BF16) for a in range(PASSES)]
 
-        wa_grouped = [round_wa(0)]
+        def round_wa(a, columns, copy):
+            copy(
+                wa_grouped[a][:].rearrange("p (t m j) -> p m j t", t=PACK, j=PACK)[:, columns],
+                wa_raw[a][:].rearrange("p j (m t) -> p m j t", t=PACK)[:, columns],
+            )
+
+        round_wa(0, slice(0, WA_SPLIT), nc.scalar.copy)
         bias_bank = bank("bias_bank", N_TILES - 1)
         nc.tensor.transpose(bias_bank[:, 0:P], bias_rows[:], identity[:])
         bias_cols = tile("bias_cols", [P, 2 * N_TILES], F32)
         nc.scalar.activation(bias_cols[:, 0:N_TILES], bias_bank[:, 0:N_TILES], IDENTITY)
-        wa_grouped.append(round_wa(1))
+        round_wa(1, slice(0, WA_SPLIT), nc.scalar.copy)
 
-        gather_words(0, 0, "tab_planes")
+        gather_words(0, 0, "scale_rows")
+        gather_words(0, 1, "tab_planes", -HALF * 4)
+        round_wa(0, slice(WA_SPLIT, P), nc.vector.tensor_copy)
         wa_q = [quantize("wa0", wa_grouped[0], R)]
-        gather_words(0, 1, "wa_grouped0")
-        gather_words(1, 0, "tab_w0")
+        round_wa(1, slice(WA_SPLIT, P), nc.vector.tensor_copy)
         wa_q.append(quantize("wa1", wa_grouped[1], R))
-        gather_words(1, 1, "tab_w0")
+        gather_words(1, 0, "wa_grouped1")
+        gather_words(1, 1, "wa_grouped1")
 
-        down_order = [(0, 0), (1, 0), (1, 1), (0, 1), (1, 2), (1, 3), (0, 2), (0, 3)]
+        down_order = [(0, 0), (0, 1), (1, 0), (1, 1), (1, 2), (1, 3), (0, 2), (0, 3)]
         down_acc = {key: bank(f"down_acc{key[0]}_{key[1]}", i) for i, key in enumerate(down_order)}
 
         def down_pass(half, j, a):
@@ -196,14 +202,17 @@ def tile_list_lora_cached_projection_kernel(
         for half in range(2):
             for j in range(PACK):
                 down_pass(half, j, 0)
-        for half, j in down_order:
-            down_pass(half, j, 1)
+        for half in range(2):
+            for j in range(PACK):
+                down_pass(half, j, 1)
 
         wb_q = {}
         wb_grouped = {}
 
-        def round_wb(c, over, copy):
-            wb_grouped[c] = tile(f"wb_grouped{c}", [P, WB_COLS * PACK], BF16, over)
+        def round_wb(c, slot, copy, grouped=None):
+            if grouped is None:
+                grouped = tile(f"wb_grouped{c}", [P, WB_COLS * PACK], BF16, "ring", slot * HALF * 4)
+            wb_grouped[c] = grouped
             copy(*interleaved_views(wb_grouped[c][:], wb_raw[c]))
 
         def quantize_wb(c, over=None, skip=0):
@@ -232,12 +241,12 @@ def tile_list_lora_cached_projection_kernel(
         h_f32 = {key: tile(f"h_f32_{key[0]}_{key[1]}", [P, 2, HALF], F32) for key in [(0, 0), (0, 1), (1, 0)]}
         down = {}
 
-        def copy_down(half, j, over=None):
-            down[half, j] = tile(f"down{half}_{j}", [P, HALF], F32, over)
-            nc.scalar.copy(down[half, j][:], down_acc[half, j][:])
+        def copy_down(half, j, slot, slots=1):
+            down[half, j] = tile(f"down{half}_{j}", [P, slots * HALF], F32, "ring", slot * HALF * 4)[:, 0:HALF]
+            nc.scalar.copy(down[half, j], down_acc[half, j][:])
 
         def scale_down(half, j):
-            nc.vector.tensor_tensor(h_f32[half, j // 2][:, j % 2, :], g_tab[j][:].indirect(picks(half)), down[half, j][:], MULT)
+            nc.vector.tensor_tensor(h_f32[half, j // 2][:, j % 2, :], g_tab[j][:].indirect(picks(half)), down[half, j], MULT)
 
         h_q = {}
 
@@ -247,10 +256,10 @@ def tile_list_lora_cached_projection_kernel(
             grouped, raw = interleaved_views(h_grouped[half][:], h_f32[half, pair][:])
             copy(grouped[:, :, 2 * pair : 2 * pair + 2, :], raw)
 
-        def quantize_h(half):
-            h_q[half] = quantize(f"h{half}", h_grouped[half], HALF)
+        def quantize_h(half, over=None, skip=0, plane=None):
+            h_q[half] = quantize(f"h{half}", h_grouped[half], HALF, over, skip, plane)
 
-        def finish(half, n, on_scalar):
+        def finish(half, n, on_scalar, over=None, skip=0):
             c, first = divmod(n * P, WB_COLS)
             codes, plane = wb_q[c]
             acc = y_acc[half, n]
@@ -263,56 +272,60 @@ def tile_list_lora_cached_projection_kernel(
                 start=False,
                 stop=True,
             )
-            result = tile(f"result{half}_{n}", [P, HALF], F32)
+            result = tile(f"result{half}_{n}", [P, HALF], F32, over, skip)
             if on_scalar:
                 nc.scalar.activation(result[:], acc[:], IDENTITY, bias=bias_cols[:, n : n + 1])
             else:
                 nc.vector.tensor_scalar(result[:], acc[:], bias_cols[:, n : n + 1], None, ADD)
             nc.sync.dma_start(out=out[n * P : (n + 1) * P, tokens(half)], in_=result[:])
 
-        for half, j in down_order[:6]:
-            copy_down(half, j)
+        place["ring"] = place["end"]
+        place["end"] += 11 * HALF * 4
+        copy_down(0, 0, 0)
+        copy_down(0, 1, 1)
+        copy_down(1, 0, 3, 3)
+        copy_down(1, 1, 6)
+        copy_down(1, 2, 7)
+        copy_down(1, 3, 8)
         scale_down(0, 0)
         scale_down(1, 0)
-        copy_down(0, 2, "down1_0")
+        copy_down(0, 2, 4, 2)
+        copy_down(0, 3, 3)
         scale_down(0, 1)
         round_h(0, 0, nc.scalar.copy)
         scale_down(1, 1)
-        copy_down(0, 3, "down1_1")
         round_h(1, 0, nc.scalar.copy)
         scale_down(0, 2)
-        round_wb(0, "down0_2", nc.scalar.copy)
+        late_planes = tile("h_f32_1_1", [P, 2 * HALF], F32)
+        h_f32[1, 1] = late_planes[:].rearrange("p (j n) -> p j n", j=2)
+        scale_down(1, 2)
+        for i in range(8):
+            base_passes(i // 4, i % 4, i)
+        round_wb(0, 5, nc.scalar.copy)
         scale_down(0, 3)
-        for a in range(PASSES):
-            for i in range(8):
-                if a == 0:
-                    y_acc[i // 4, i % 4] = bank(f"y_acc{i // 4}_{i % 4}", i)
-                base_pass(i // 4, i % 4, a)
-        round_wb(1, "down0_3", nc.scalar.copy)
+        round_wb(1, None, nc.scalar.copy, late_planes[:, HALF:].bitcast(BF16))
         round_h(0, 1, nc.vector.tensor_copy)
         quantize_wb(0)
-        quantize_h(0)
+        quantize_h(0, "ring", 5 * HALF * 4)
         quantize_wb(1)
-        h_f32[1, 1] = tile("h_f32_1_1", [P, 2, HALF], F32, "down1_1")
-        scale_down(1, 2)
-        wb_grouped[2] = h_f32[1, 1][:, 1, :].bitcast(BF16)
-        nc.vector.tensor_copy(*interleaved_views(wb_grouped[2], wb_raw[2]))
-        quantize_wb(2)
+        round_wb(2, 3, nc.vector.tensor_copy)
         scale_down(1, 3)
+        quantize_wb(2)
+        round_wb(3, 8, nc.vector.tensor_copy)
         for n in range(4):
             finish(0, n, True)
-        for n in range(4, 8):
+        for n in range(4, 6):
             base_passes(0, n, n - 4)
-        round_wb(3, "down1_2", nc.scalar.copy)
-        finish(0, 4, True)
-        finish(0, 5, True)
-        quantize_wb(3)
-        round_h(1, 1, nc.vector.tensor_copy)
-        quantize_h(1)
+            finish(0, n, True)
+        for n in range(6, 8):
+            base_passes(0, n, n - 4)
         base_passes(1, 4, 0)
+        round_h(1, 1, nc.vector.tensor_copy)
+        quantize_wb(3)
         finish(0, 6, True)
         finish(0, 7, True)
         base_passes(1, 5, 1)
+        quantize_h(1, "ring", 8 * HALF * 4)
         for n in range(4):
             finish(1, n, n % 2 == 1)
         base_passes(1, 6, 2)

@@ -136,7 +136,7 @@ def tile_list_lora_cached_projection_kernel(
             nc.sync.dma_start(out=moved_plane[r:P:32, :], in_=v_plane[4 + r : P : 32, :].bitcast(I32))
         load_wb(0, 1)
         load_wb(1, 1)
-        load_wb(2, 1)
+        load_wb(2, 1, PACK)
         load_wb(3, 1)
         load_w4(1)
 
@@ -245,8 +245,12 @@ def tile_list_lora_cached_projection_kernel(
             down[half, j] = tile(f"down{half}_{j}", [P, slots * HALF], F32, "ring", slot * HALF * 4)[:, 0:HALF]
             nc.scalar.copy(down[half, j], down_acc[half, j][:])
 
-        def scale_down(half, j):
-            nc.vector.tensor_tensor(h_f32[half, j // 2][:, j % 2, :], g_tab[j][:].indirect(picks(half)), down[half, j], MULT)
+        def scale_down(half, j, first=0, count=HALF):
+            cols = slice(first, first + count)
+            entries = offsets[:, (half * HALF + first) // 16 : (half * HALF + first + count) // 16]
+            nc.vector.tensor_tensor(
+                h_f32[half, j // 2][:, j % 2, cols], g_tab[j][:].indirect(entries), down[half, j][:, cols], MULT
+            )
 
         h_q = {}
 
@@ -298,37 +302,38 @@ def tile_list_lora_cached_projection_kernel(
         scale_down(0, 2)
         late_planes = tile("h_f32_1_1", [P, 2 * HALF], F32)
         h_f32[1, 1] = late_planes[:].rearrange("p (j n) -> p j n", j=2)
-        scale_down(1, 2)
+        scale_down(1, 2, 0, HALF // 2)
         for i in range(8):
             base_passes(i // 4, i % 4, i)
         round_wb(0, 5, nc.scalar.copy)
         scale_down(0, 3)
-        round_wb(1, None, nc.scalar.copy, late_planes[:, HALF:].bitcast(BF16))
+        round_wb(1, None, nc.scalar.copy, late_planes[:, HALF // 2 : 3 * HALF // 2].bitcast(BF16))
+        round_wb(2, 9, nc.scalar.copy)
         round_h(0, 1, nc.vector.tensor_copy)
         quantize_wb(0)
         quantize_h(0, "ring", 5 * HALF * 4)
         quantize_wb(1)
-        round_wb(2, 3, nc.vector.tensor_copy)
-        scale_down(1, 3)
         quantize_wb(2)
-        round_wb(3, 8, nc.vector.tensor_copy)
+        round_wb(3, None, nc.vector.tensor_copy, late_planes[:, HALF:].bitcast(BF16))
+        scale_down(1, 2, HALF // 2, HALF // 2)
+        quantize_wb(3)
+        scale_down(1, 3)
         for n in range(4):
-            finish(0, n, True)
+            finish(0, n, True, "wb_raw2", n * HALF * 4)
         for n in range(4, 6):
             base_passes(0, n, n - 4)
             finish(0, n, True)
         for n in range(6, 8):
-            base_passes(0, n, n - 4)
+            y_acc[0, n] = bank(f"y_acc0_{n}", n - 4)
+            base_pass(0, n, 0)
+        for n in range(6, 8):
+            base_pass(0, n, 1)
+            finish(0, n, True)
         base_passes(1, 4, 0)
         round_h(1, 1, nc.vector.tensor_copy)
-        quantize_wb(3)
-        finish(0, 6, True)
-        finish(0, 7, True)
-        base_passes(1, 5, 1)
-        quantize_h(1, "ring", 8 * HALF * 4)
-        for n in range(4):
+        quantize_h(1, "v_codes0_0")
+        for n in range(5):
             finish(1, n, n % 2 == 1)
-        base_passes(1, 6, 2)
-        base_passes(1, 7, 3)
-        for n in range(4, 8):
+        for n in range(5, 8):
+            base_passes(1, n, n - 4)
             finish(1, n, n % 2 == 1)

@@ -26,7 +26,7 @@ PASSES = K // (P * PACK)
 HALF = 512
 N_TILES = N // P
 WB_COLS = 256
-WA_SPLIT = 48
+WA_SPLIT = (96, 80)
 
 
 def tile_list_lora_cached_projection_kernel(
@@ -167,24 +167,25 @@ def tile_list_lora_cached_projection_kernel(
                 wa_raw[a][:].rearrange("p j (m t) -> p m j t", t=PACK)[:, columns],
             )
 
-        round_wa(0, slice(0, WA_SPLIT), nc.scalar.copy)
+        round_wa(0, slice(0, WA_SPLIT[0]), nc.scalar.copy)
         bias_bank = bank("bias_bank", N_TILES - 1)
         nc.tensor.transpose(bias_bank[:, 0:P], bias_rows[:], identity[:])
         bias_cols = tile("bias_cols", [P, 2 * N_TILES], F32)
         nc.scalar.activation(bias_cols[:, 0:N_TILES], bias_bank[:, 0:N_TILES], IDENTITY)
-        round_wa(1, slice(0, WA_SPLIT), nc.scalar.copy)
+        round_wa(1, slice(0, WA_SPLIT[1]), nc.scalar.copy)
 
         gather_words(0, 0, "scale_rows")
         gather_words(0, 1, "tab_planes", -HALF * 4)
-        round_wa(0, slice(WA_SPLIT, P), nc.vector.tensor_copy)
+        round_wa(0, slice(WA_SPLIT[0], P), nc.vector.tensor_copy)
         wa_q = [quantize("wa0", wa_grouped[0], R)]
-        round_wa(1, slice(WA_SPLIT, P), nc.vector.tensor_copy)
+        round_wa(1, slice(WA_SPLIT[1], P), nc.vector.tensor_copy)
         wa_q.append(quantize("wa1", wa_grouped[1], R))
         gather_words(1, 0, "wa_grouped1")
         gather_words(1, 1, "wa_grouped1")
 
-        down_order = [(0, 0), (0, 1), (1, 0), (1, 1), (1, 2), (1, 3), (0, 2), (0, 3)]
-        down_acc = {key: bank(f"down_acc{key[0]}_{key[1]}", i) for i, key in enumerate(down_order)}
+        early = [(0, 0), (0, 1), (1, 0), (1, 1), (0, 2)]
+        late = [(1, 2), (0, 3), (1, 3)]
+        down_acc = {key: bank(f"down_acc{key[0]}_{key[1]}", i) for i, key in enumerate(early)}
 
         def down_pass(half, j, a):
             codes, plane = wa_q[a]
@@ -199,12 +200,9 @@ def tile_list_lora_cached_projection_kernel(
                 stop=(a == PASSES - 1),
             )
 
-        for half in range(2):
-            for j in range(PACK):
-                down_pass(half, j, 0)
-        for half in range(2):
-            for j in range(PACK):
-                down_pass(half, j, 1)
+        for a in range(PASSES):
+            for half, j in early:
+                down_pass(half, j, a)
 
         wb_q = {}
         wb_grouped = {}
@@ -283,12 +281,17 @@ def tile_list_lora_cached_projection_kernel(
                 nc.vector.tensor_scalar(result[:], acc[:], bias_cols[:, n : n + 1], None, ADD)
             nc.sync.dma_start(out=out[n * P : (n + 1) * P, tokens(half)], in_=result[:])
 
+        first_banks = [5, 6, 7, 3, 4, 0, 2, 1]
         place["ring"] = place["end"]
         place["end"] += 11 * HALF * 4
         copy_down(0, 0, 0)
         copy_down(0, 1, 1)
         copy_down(1, 0, 3, 3)
         copy_down(1, 1, 6)
+        for i, (half, j) in enumerate(late):
+            down_acc[half, j] = bank(f"down_acc{half}_{j}", i)
+            for a in range(PASSES):
+                down_pass(half, j, a)
         copy_down(1, 2, 7)
         copy_down(1, 3, 8)
         scale_down(0, 0)
@@ -304,7 +307,7 @@ def tile_list_lora_cached_projection_kernel(
         h_f32[1, 1] = late_planes[:].rearrange("p (j n) -> p j n", j=2)
         scale_down(1, 2, 0, HALF // 2)
         for i in range(8):
-            base_passes(i // 4, i % 4, i)
+            base_passes(i // 4, i % 4, first_banks[i])
         round_wb(0, 5, nc.scalar.copy)
         scale_down(0, 3)
         round_wb(1, None, nc.scalar.copy, late_planes[:, HALF // 2 : 3 * HALF // 2].bitcast(BF16))
@@ -321,19 +324,19 @@ def tile_list_lora_cached_projection_kernel(
         for n in range(4):
             finish(0, n, True, "wb_raw2", n * HALF * 4)
         for n in range(4, 6):
-            base_passes(0, n, n - 4)
+            base_passes(0, n, first_banks[n - 4])
             finish(0, n, True)
         for n in range(6, 8):
-            y_acc[0, n] = bank(f"y_acc0_{n}", n - 4)
+            y_acc[0, n] = bank(f"y_acc0_{n}", first_banks[n - 4])
             base_pass(0, n, 0)
         for n in range(6, 8):
             base_pass(0, n, 1)
             finish(0, n, True)
-        base_passes(1, 4, 0)
+        base_passes(1, 4, first_banks[0])
         round_h(1, 1, nc.vector.tensor_copy)
         quantize_h(1, "v_codes0_0")
         for n in range(5):
             finish(1, n, n % 2 == 1)
         for n in range(5, 8):
-            base_passes(1, n, n - 4)
+            base_passes(1, n, first_banks[n - 4])
             finish(1, n, n % 2 == 1)

@@ -23,10 +23,11 @@ ELEMENT_BYTES = {F32: 4, I32: 4, U32: 4, BF16: 2, U8: 1}
 P = 128
 PACK = 4
 PASSES = K // (P * PACK)
-HALF = 512
+BANK = 512
 N_TILES = N // P
 WB_COLS = 256
-WA_SPLIT = (96, 80)
+WA_ON_SCALAR = (72, 60)
+PIECES = {"A": (0, 512), "B": (512, 256), "C": (768, 256)}
 
 
 def tile_list_lora_cached_projection_kernel(
@@ -49,23 +50,12 @@ def tile_list_lora_cached_projection_kernel(
             return sbuf.tile(shape, dtype, name=name, offset=place[name], align_bytes=64)
 
         def bank(name, number):
-            return psum.tile([P, HALF], F32, name=name, tag=f"bank{number}")
+            return psum.tile([P, BANK], F32, name=name, tag=f"bank{number}")
 
         offsets = lists.tile([P, S // 16], U16, name="offsets")
 
-        def picks(half):
-            return offsets[:, half * (HALF // 16) : (half + 1) * (HALF // 16)]
-
-        def tokens(half):
-            return slice(half * HALF, (half + 1) * HALF)
-
-        wa_raw = [tile(f"wa_raw{a}", [P, PACK, R], F32) for a in range(PASSES)]
-
-        def load_wa(a):
-            nc.sync.dma_start(
-                out=wa_raw[a][:],
-                in_=wa[a * P * PACK : (a + 1) * P * PACK, :].rearrange("(p j) r -> p j r", j=PACK),
-            )
+        def picks(first, count):
+            return offsets[:, first // 16 : (first + count) // 16]
 
         scale_rows = tile("scale_rows", [P, T // 4], I32)
         for q in range(4):
@@ -88,28 +78,31 @@ def tile_list_lora_cached_projection_kernel(
         make_identity(nc, identity[:])
 
         tab_w = [tile(f"tab_w{a}", [P, T], I32) for a in range(PASSES)]
-        w4_tiles = [tile(f"w4_codes{u}", [P, (2 * PASSES * N // 2) + 2 * P], U8) for u in range(2)]
-        w4_codes = [t[:, 2 * P :].rearrange("p (a b) -> p a b", a=PASSES) for t in w4_tiles]
+        wa_raw = [tile(f"wa_raw{a}", [P, PACK, R], F32) for a in range(PASSES)]
+        w4_codes = [tile(f"w4_codes{u}", [P, PASSES, N], U8) for u in range(2)]
         g_tab = [tile(f"g_tab{j}", [P, T], F32) for j in range(PACK)]
-        wb_raw = {}
+        wb_raw = [tile(f"wb_raw{c}", [P, PACK, WB_COLS], F32) for c in range(N // WB_COLS)]
 
         def load_words(a):
             nc.sync.dma_start(out=tab_w[a][:], in_=tab_words[a].rearrange("p t i -> p (t i)").bitcast(I32))
 
+        def load_wa(a):
+            nc.sync.dma_start(
+                out=wa_raw[a][:],
+                in_=wa[a * P * PACK : (a + 1) * P * PACK, :].rearrange("(p j) r -> p j r", j=PACK),
+            )
+
         def load_w4(u):
             nc.sync.dma_start(
-                out=w4_codes[u].bitcast(I32),
+                out=w4_codes[u][:].bitcast(I32),
                 in_=w4_words[:, :, u * N : (u + 1) * N].rearrange("a p b -> p a b").bitcast(I32),
             )
 
-        def load_wb(first, count, spare=0):
-            raw = tile(f"wb_raw{first}", [P, PACK + spare, count * WB_COLS], F32)[:, 0:PACK, :]
+        def load_wb(c):
             nc.sync.dma_start(
-                out=raw,
-                in_=wb[:, first * WB_COLS : (first + count) * WB_COLS].rearrange("(p j) n -> p j n", j=PACK),
+                out=wb_raw[c][:],
+                in_=wb[:, c * WB_COLS : (c + 1) * WB_COLS].rearrange("(p j) n -> p j n", j=PACK),
             )
-            for c in range(count):
-                wb_raw[first + c] = raw[:, :, c * WB_COLS : (c + 1) * WB_COLS]
 
         def load_g(j):
             nc.sync.dma_start(out=g_tab[j][:], in_=gT.rearrange("(p j) t -> j p t", j=PACK)[j])
@@ -129,16 +122,16 @@ def tile_list_lora_cached_projection_kernel(
                 in_=w4_scales[:, r:16:4, :].rearrange("a q c -> q a c").bitcast(I32),
             )
         load_g(1)
-        load_w4(0)
         load_g(2)
+        load_w4(0)
         load_g(3)
         for r in range(4):
             nc.sync.dma_start(out=moved_plane[r:P:32, :], in_=v_plane[4 + r : P : 32, :].bitcast(I32))
-        load_wb(0, 1)
-        load_wb(1, 1)
-        load_wb(2, 1, PACK)
-        load_wb(3, 1)
+        load_wb(0)
+        load_wb(1)
+        load_wb(2)
         load_w4(1)
+        load_wb(3)
 
         def interleaved_views(grouped, raw):
             return (
@@ -146,18 +139,17 @@ def tile_list_lora_cached_projection_kernel(
                 raw.rearrange("p j (c i) -> p c j i", i=4),
             )
 
-        def quantize(name, grouped, cols, over=None, skip=0, plane=None):
+        def quantize(name, grouped, cols, over=None, skip=0):
             codes = tile(name + "_codes", [P, cols], U32, over, skip)
-            if plane is None:
-                plane = tile(name + "_plane", [P, cols], U8)
+            plane = tile(name + "_plane", [P, cols], U8)
             nc.vector.quantize_mx(out=codes[:].bitcast(FP8X4), scales=plane[:], in_=grouped[:])
             return codes, plane
 
         v_codes = {}
 
         def gather_words(a, half, over, skip=0):
-            v_codes[a, half] = tile(f"v_codes{a}_{half}", [P, HALF], U32, over, half * HALF * 4 + skip)
-            nc.vector.tensor_copy(v_codes[a, half][:], tab_w[a][:].bitcast(U32).indirect(picks(half)))
+            v_codes[a, half] = tile(f"v_codes{a}_{half}", [P, BANK], U32, over, skip)
+            nc.vector.tensor_copy(v_codes[a, half][:], tab_w[a][:].bitcast(U32).indirect(picks(half * BANK, BANK)))
 
         wa_grouped = [tile(f"wa_grouped{a}", [P, R * PACK], BF16) for a in range(PASSES)]
 
@@ -167,24 +159,24 @@ def tile_list_lora_cached_projection_kernel(
                 wa_raw[a][:].rearrange("p j (m t) -> p m j t", t=PACK)[:, columns],
             )
 
-        round_wa(0, slice(0, WA_SPLIT[0]), nc.scalar.copy)
+        round_wa(0, slice(0, WA_ON_SCALAR[0]), nc.scalar.copy)
         bias_bank = bank("bias_bank", N_TILES - 1)
         nc.tensor.transpose(bias_bank[:, 0:P], bias_rows[:], identity[:])
         bias_cols = tile("bias_cols", [P, 2 * N_TILES], F32)
         nc.scalar.activation(bias_cols[:, 0:N_TILES], bias_bank[:, 0:N_TILES], IDENTITY)
-        round_wa(1, slice(0, WA_SPLIT[1]), nc.scalar.copy)
+        round_wa(1, slice(0, WA_ON_SCALAR[1]), nc.scalar.copy)
 
         gather_words(0, 0, "scale_rows")
-        gather_words(0, 1, "tab_planes", -HALF * 4)
-        round_wa(0, slice(WA_SPLIT[0], P), nc.vector.tensor_copy)
+        gather_words(0, 1, "tab_planes")
+        round_wa(0, slice(WA_ON_SCALAR[0], P), nc.vector.tensor_copy)
         wa_q = [quantize("wa0", wa_grouped[0], R)]
-        round_wa(1, slice(WA_SPLIT[1], P), nc.vector.tensor_copy)
+        round_wa(1, slice(WA_ON_SCALAR[1], P), nc.vector.tensor_copy)
         wa_q.append(quantize("wa1", wa_grouped[1], R))
         gather_words(1, 0, "wa_grouped1")
-        gather_words(1, 1, "wa_grouped1")
+        gather_words(1, 1, "wa_grouped1", BANK * 4)
 
-        early = [(0, 0), (0, 1), (1, 0), (1, 1), (0, 2)]
-        late = [(1, 2), (0, 3), (1, 3)]
+        early = [(0, 0), (1, 0), (0, 1), (1, 1), (0, 2)]
+        late = [(0, 3), (1, 2), (1, 3)]
         down_acc = {key: bank(f"down_acc{key[0]}_{key[1]}", i) for i, key in enumerate(early)}
 
         def down_pass(half, j, a):
@@ -195,148 +187,170 @@ def tile_list_lora_cached_projection_kernel(
                 lhsT=codes[:, cols].bitcast(FP8X4),
                 lhsT_scale=plane[:, cols],
                 rhs=v_codes[a, half][:].bitcast(FP8X4),
-                rhs_scale=v_plane[4 * a : P, tokens(half)],
+                rhs_scale=v_plane[4 * a : P, half * BANK : (half + 1) * BANK],
                 start=(a == 0),
                 stop=(a == PASSES - 1),
             )
 
+        down = {}
+
+        def copy_down(half, j):
+            down[half, j] = tile(f"down{half}_{j}", [P, BANK], F32)
+            nc.scalar.copy(down[half, j][:], down_acc[half, j][:])
+
         for a in range(PASSES):
             for half, j in early:
                 down_pass(half, j, a)
-
-        wb_q = {}
-        wb_grouped = {}
-
-        def round_wb(c, slot, copy, grouped=None):
-            if grouped is None:
-                grouped = tile(f"wb_grouped{c}", [P, WB_COLS * PACK], BF16, "ring", slot * HALF * 4)
-            wb_grouped[c] = grouped
-            copy(*interleaved_views(wb_grouped[c][:], wb_raw[c]))
-
-        def quantize_wb(c, over=None, skip=0):
-            wb_q[c] = quantize(f"wb{c}", wb_grouped[c], WB_COLS, over, skip)
-
-        y_acc = {}
-
-        def base_pass(half, n, a):
-            u, c = divmod(n, N_TILES // 2)
-            scales = v_plane[:] if a == 0 else moved_plane[:].bitcast(U8)
-            nc.tensor.matmul_mx(
-                out=y_acc[half, n][:],
-                lhsT=w4_codes[u][:, a, 2 * c * P : 2 * (c + 1) * P].bitcast(FP4X4),
-                lhsT_scale=w4_planes[:, a, :].bitcast(U8)[:, n * P : (n + 1) * P],
-                rhs=v_codes[a, half][:].bitcast(FP8X4),
-                rhs_scale=scales[:, tokens(half)],
-                start=(a == 0),
-                stop=False,
-            )
-
-        def base_passes(half, n, number):
-            y_acc[half, n] = bank(f"y_acc{half}_{n}", number)
-            for a in range(PASSES):
-                base_pass(half, n, a)
-
-        h_f32 = {key: tile(f"h_f32_{key[0]}_{key[1]}", [P, 2, HALF], F32) for key in [(0, 0), (0, 1), (1, 0)]}
-        down = {}
-
-        def copy_down(half, j, slot, slots=1):
-            down[half, j] = tile(f"down{half}_{j}", [P, slots * HALF], F32, "ring", slot * HALF * 4)[:, 0:HALF]
-            nc.scalar.copy(down[half, j], down_acc[half, j][:])
-
-        def scale_down(half, j, first=0, count=HALF):
-            cols = slice(first, first + count)
-            entries = offsets[:, (half * HALF + first) // 16 : (half * HALF + first + count) // 16]
-            nc.vector.tensor_tensor(
-                h_f32[half, j // 2][:, j % 2, cols], g_tab[j][:].indirect(entries), down[half, j][:, cols], MULT
-            )
-
-        h_q = {}
-
-        h_grouped = [tile(f"h_grouped{half}", [P, HALF * PACK], BF16, None) for half in range(2)]
-
-        def round_h(half, pair, copy):
-            grouped, raw = interleaved_views(h_grouped[half][:], h_f32[half, pair][:])
-            copy(grouped[:, :, 2 * pair : 2 * pair + 2, :], raw)
-
-        def quantize_h(half, over=None, skip=0, plane=None):
-            h_q[half] = quantize(f"h{half}", h_grouped[half], HALF, over, skip, plane)
-
-        def finish(half, n, on_scalar, over=None, skip=0):
-            c, first = divmod(n * P, WB_COLS)
-            codes, plane = wb_q[c]
-            acc = y_acc[half, n]
-            nc.tensor.matmul_mx(
-                out=acc[:],
-                lhsT=codes[:, first : first + P].bitcast(FP8X4),
-                lhsT_scale=plane[:, first : first + P],
-                rhs=h_q[half][0][:].bitcast(FP8X4),
-                rhs_scale=h_q[half][1][:],
-                start=False,
-                stop=True,
-            )
-            result = tile(f"result{half}_{n}", [P, HALF], F32, over, skip)
-            if on_scalar:
-                nc.scalar.activation(result[:], acc[:], IDENTITY, bias=bias_cols[:, n : n + 1])
-            else:
-                nc.vector.tensor_scalar(result[:], acc[:], bias_cols[:, n : n + 1], None, ADD)
-            nc.sync.dma_start(out=out[n * P : (n + 1) * P, tokens(half)], in_=result[:])
-
-        first_banks = [5, 6, 7, 3, 4, 0, 2, 1]
-        place["ring"] = place["end"]
-        place["end"] += 11 * HALF * 4
-        copy_down(0, 0, 0)
-        copy_down(0, 1, 1)
-        copy_down(1, 0, 3, 3)
-        copy_down(1, 1, 6)
+        for half, j in early[: len(late)]:
+            copy_down(half, j)
         for i, (half, j) in enumerate(late):
             down_acc[half, j] = bank(f"down_acc{half}_{j}", i)
             for a in range(PASSES):
                 down_pass(half, j, a)
-        copy_down(1, 2, 7)
-        copy_down(1, 3, 8)
-        scale_down(0, 0)
-        scale_down(1, 0)
-        copy_down(0, 2, 4, 2)
-        copy_down(0, 3, 3)
-        scale_down(0, 1)
-        round_h(0, 0, nc.scalar.copy)
-        scale_down(1, 1)
-        round_h(1, 0, nc.scalar.copy)
-        scale_down(0, 2)
-        late_planes = tile("h_f32_1_1", [P, 2 * HALF], F32)
-        h_f32[1, 1] = late_planes[:].rearrange("p (j n) -> p j n", j=2)
-        scale_down(1, 2, 0, HALF // 2)
-        for i in range(8):
-            base_passes(i // 4, i % 4, first_banks[i])
-        round_wb(0, 5, nc.scalar.copy)
-        scale_down(0, 3)
-        round_wb(1, None, nc.scalar.copy, late_planes[:, HALF // 2 : 3 * HALF // 2].bitcast(BF16))
-        round_wb(2, 9, nc.scalar.copy)
-        round_h(0, 1, nc.vector.tensor_copy)
+        for half, j in early[len(late) :] + late:
+            copy_down(half, j)
+
+        h_f32 = {}
+        h_grouped = {piece: tile(f"h_grouped{piece}", [P, count * PACK], BF16) for piece, (first, count) in PIECES.items()}
+        h_q = {}
+
+        def scale_down(dst, j, first, count):
+            half, inner = divmod(first, BANK)
+            nc.vector.tensor_tensor(
+                dst, g_tab[j][:].indirect(picks(first, count)), down[half, j][:, inner : inner + count], MULT
+            )
+
+        def round_h(piece, pair, copy):
+            grouped, raw = interleaved_views(h_grouped[piece][:], h_f32[piece, pair])
+            copy(grouped[:, :, 2 * pair : 2 * pair + 2, :], raw)
+
+        def quantize_h(piece, over=None):
+            h_q[piece] = quantize(f"h{piece}", h_grouped[piece], PIECES[piece][1], over)
+
+        first_pairs = [tile(f"h_first{half}", [P, 2, BANK], F32) for half in range(2)]
+        for j in range(2):
+            for half in range(2):
+                scale_down(first_pairs[half][:, j, :], j, half * BANK, BANK)
+        for piece, (first, count) in PIECES.items():
+            half, inner = divmod(first, BANK)
+            h_f32[piece, 0] = first_pairs[half][:, :, inner : inner + count]
+            round_h(piece, 0, nc.scalar.copy)
+
+        def second_pair(piece, j, over=None):
+            first, count = PIECES[piece]
+            if j == 2:
+                h_f32[piece, 1] = tile(f"h_second{piece}", [P, 2, count], F32, over)[:]
+            scale_down(h_f32[piece, 1][:, j - 2, :], j, first, count)
+
+        wb_q = {}
+        wb_grouped = {}
+
+        def round_wb(c, copy, over=None):
+            wb_grouped[c] = tile(f"wb_grouped{c}", [P, WB_COLS * PACK], BF16, over)
+            copy(*interleaved_views(wb_grouped[c][:], wb_raw[c][:]))
+
+        def quantize_wb(c):
+            wb_q[c] = quantize(f"wb{c}", wb_grouped[c], WB_COLS)
+
+        y_acc = {}
+
+        def columns(piece, rows, n):
+            count = PIECES[piece][1]
+            return slice((n - rows[0]) * count, (n - rows[0] + 1) * count)
+
+        def base_passes(piece, rows, a, number=None):
+            if a == 0:
+                y_acc[piece, rows] = bank(f"y_acc{piece}{rows[0]}", number)
+            first, count = PIECES[piece]
+            half, inner = divmod(first, BANK)
+            scales = v_plane[:] if a == 0 else moved_plane[:].bitcast(U8)
+            for n in rows:
+                u, c = divmod(n, N_TILES // 2)
+                nc.tensor.matmul_mx(
+                    out=y_acc[piece, rows][:, columns(piece, rows, n)],
+                    lhsT=w4_codes[u][:, a, 2 * c * P : 2 * (c + 1) * P].bitcast(FP4X4),
+                    lhsT_scale=w4_planes[:, a, :].bitcast(U8)[:, n * P : (n + 1) * P],
+                    rhs=v_codes[a, half][:, inner : inner + count].bitcast(FP8X4),
+                    rhs_scale=scales[:, first : first + count],
+                    start=(a == 0 and n == rows[0]),
+                    stop=False,
+                )
+
+        def both_base_passes(piece, rows, number):
+            base_passes(piece, rows, 0, number)
+            base_passes(piece, rows, 1)
+
+        def finish(piece, rows, on_scalar=True, over=None, skip=0):
+            first, count = PIECES[piece]
+            acc = y_acc[piece, rows]
+            for n in rows:
+                c, col = divmod(n * P, WB_COLS)
+                codes, plane = wb_q[c]
+                nc.tensor.matmul_mx(
+                    out=acc[:, columns(piece, rows, n)],
+                    lhsT=codes[:, col : col + P].bitcast(FP8X4),
+                    lhsT_scale=plane[:, col : col + P],
+                    rhs=h_q[piece][0][:].bitcast(FP8X4),
+                    rhs_scale=h_q[piece][1][:],
+                    start=False,
+                    stop=(n == rows[-1]),
+                )
+            result = tile(f"result{piece}{rows[0]}", [P, len(rows) * count], F32, over, skip)
+            for n in rows:
+                cols = columns(piece, rows, n)
+                if on_scalar:
+                    nc.scalar.activation(result[:, cols], acc[:, cols], IDENTITY, bias=bias_cols[:, n : n + 1])
+                else:
+                    nc.vector.tensor_scalar(result[:, cols], acc[:, cols], bias_cols[:, n : n + 1], None, ADD)
+            nc.sync.dma_start(
+                out=out[rows[0] * P : (rows[-1] + 1) * P, first : first + count].rearrange("(c p) t -> p c t", p=P),
+                in_=result[:].rearrange("p (c t) -> p c t", t=count),
+            )
+
+        prefilled = [("A", (n,)) for n in range(4)] + [(piece, rows) for piece in "BC" for rows in ((0, 1), (2, 3))]
+        banks = dict(zip(prefilled, [5, 6, 7, 3, 4, 0, 1, 2]))
+        second_pair("A", 2)
+        for key in prefilled:
+            base_passes(*key, 0, banks[key])
+        for key in prefilled:
+            base_passes(*key, 1)
+        round_wb(0, nc.scalar.copy)
+        second_pair("A", 3)
+        round_wb(1, nc.scalar.copy)
+        round_h("A", 1, nc.vector.tensor_copy)
+        quantize_h("A")
         quantize_wb(0)
-        quantize_h(0, "ring", 5 * HALF * 4)
         quantize_wb(1)
+        for n in range(2):
+            finish("A", (n,), True, "wb_raw1", n * BANK * 4)
+        round_wb(2, nc.vector.tensor_copy, "wb_grouped1")
+        round_wb(3, nc.vector.tensor_copy)
         quantize_wb(2)
-        round_wb(3, None, nc.vector.tensor_copy, late_planes[:, HALF:].bitcast(BF16))
-        scale_down(1, 2, HALF // 2, HALF // 2)
         quantize_wb(3)
-        scale_down(1, 3)
-        for n in range(4):
-            finish(0, n, True, "wb_raw2", n * HALF * 4)
-        for n in range(4, 6):
-            base_passes(0, n, first_banks[n - 4])
-            finish(0, n, True)
-        for n in range(6, 8):
-            y_acc[0, n] = bank(f"y_acc0_{n}", first_banks[n - 4])
-            base_pass(0, n, 0)
-        for n in range(6, 8):
-            base_pass(0, n, 1)
-            finish(0, n, True)
-        base_passes(1, 4, first_banks[0])
-        round_h(1, 1, nc.vector.tensor_copy)
-        quantize_h(1, "v_codes0_0")
-        for n in range(5):
-            finish(1, n, n % 2 == 1)
-        for n in range(5, 8):
-            base_passes(1, n, first_banks[n - 4])
-            finish(1, n, n % 2 == 1)
+        second_pair("B", 2, "wb_raw3")
+        for n in range(2, 4):
+            finish("A", (n,))
+        for n in range(4, 8):
+            both_base_passes("A", (n,), banks["A", (n - 4,)])
+            finish("A", (n,))
+        second_pair("B", 3)
+        round_h("B", 1, nc.vector.tensor_copy)
+        quantize_h("B")
+        second_pair("C", 2, "h_groupedB")
+        for rows in ((0, 1), (2, 3)):
+            finish("B", rows)
+        both_base_passes("B", (4, 5), banks["A", (0,)])
+        finish("B", (4, 5))
+        second_pair("C", 3)
+        round_h("C", 1, nc.vector.tensor_copy)
+        quantize_h("C")
+        both_base_passes("B", (6, 7), banks["A", (1,)])
+        finish("B", (6, 7), False)
+        both_base_passes("C", (4, 5), banks["A", (2,)])
+        finish("C", (0, 1), False)
+        finish("C", (2, 3))
+        finish("C", (4, 5))
+        both_base_passes("C", (6,), banks["A", (3,)])
+        finish("C", (6,), False)
+        both_base_passes("C", (7,), banks["B", (0, 1)])
+        finish("C", (7,), False)

@@ -81,7 +81,9 @@ def tile_list_lora_cached_projection_kernel(
         wa_raw = [tile(f"wa_raw{a}", [P, PACK, R], F32) for a in range(PASSES)]
         w4_codes = [tile(f"w4_codes{u}", [P, PASSES, N], U8) for u in range(2)]
         g_tab = [tile(f"g_tab{j}", [P, T], F32) for j in range(PACK)]
-        wb_raw = [tile(f"wb_raw{c}", [P, PACK, WB_COLS], F32) for c in range(N // WB_COLS)]
+        wb_raw = [
+            tile(f"wb_raw{c}", [P, PACK + (2 if c == 1 else 0), WB_COLS], F32)[:, 0:PACK, :] for c in range(N // WB_COLS)
+        ]
 
         def load_words(a):
             nc.sync.dma_start(out=tab_w[a][:], in_=tab_words[a].rearrange("p t i -> p (t i)").bitcast(I32))
@@ -100,7 +102,7 @@ def tile_list_lora_cached_projection_kernel(
 
         def load_wb(c):
             nc.sync.dma_start(
-                out=wb_raw[c][:],
+                out=wb_raw[c],
                 in_=wb[:, c * WB_COLS : (c + 1) * WB_COLS].rearrange("(p j) n -> p j n", j=PACK),
             )
 
@@ -139,17 +141,28 @@ def tile_list_lora_cached_projection_kernel(
                 raw.rearrange("p j (c i) -> p c j i", i=4),
             )
 
-        def quantize(name, grouped, cols, over=None, skip=0):
-            codes = tile(name + "_codes", [P, cols], U32, over, skip)
+        def quantize(name, grouped, cols, cuts=1):
+            codes = tile(name + "_codes", [P, cols], U32)
             plane = tile(name + "_plane", [P, cols], U8)
-            nc.vector.quantize_mx(out=codes[:].bitcast(FP8X4), scales=plane[:], in_=grouped[:])
+            count = cols // cuts
+            for first in range(0, cols, count):
+                nc.vector.quantize_mx(
+                    out=codes[:, first : first + count].bitcast(FP8X4),
+                    scales=plane[:, first : first + count],
+                    in_=grouped[:, first * PACK : (first + count) * PACK],
+                )
             return codes, plane
 
         v_codes = {}
 
-        def gather_words(a, half, over, skip=0):
+        def gather_words(a, half, over, skip=0, cuts=1):
             v_codes[a, half] = tile(f"v_codes{a}_{half}", [P, BANK], U32, over, skip)
-            nc.vector.tensor_copy(v_codes[a, half][:], tab_w[a][:].bitcast(U32).indirect(picks(half * BANK, BANK)))
+            count = BANK // cuts
+            for inner in range(0, BANK, count):
+                nc.vector.tensor_copy(
+                    v_codes[a, half][:, inner : inner + count],
+                    tab_w[a][:].bitcast(U32).indirect(picks(half * BANK + inner, count)),
+                )
 
         wa_grouped = [tile(f"wa_grouped{a}", [P, R * PACK], BF16) for a in range(PASSES)]
 
@@ -172,82 +185,90 @@ def tile_list_lora_cached_projection_kernel(
         wa_q = [quantize("wa0", wa_grouped[0], R)]
         round_wa(1, slice(WA_ON_SCALAR[1], P), nc.vector.tensor_copy)
         wa_q.append(quantize("wa1", wa_grouped[1], R))
-        gather_words(1, 0, "wa_grouped1")
+        gather_words(1, 0, "wa_grouped1", 0, 2)
         gather_words(1, 1, "wa_grouped1", BANK * 4)
 
-        early = [(0, 0), (1, 0), (0, 1), (1, 1), (0, 2)]
-        late = [(0, 3), (1, 2), (1, 3)]
-        down_acc = {key: bank(f"down_acc{key[0]}_{key[1]}", i) for i, key in enumerate(early)}
+        early = [(0, 256, 0), (256, 256, 0), (512, 512, 0), (0, 512, 1), (512, 512, 1), (0, 512, 2)]
+        late = [(0, 512, 3), (512, 512, 2), (512, 512, 3)]
+        down_acc = {key: bank(f"down_acc{key[0]}_{key[2]}", i) for i, key in enumerate(early)}
 
-        def down_pass(half, j, a):
+        def down_pass(first, count, j, a):
             codes, plane = wa_q[a]
+            half, inner = divmod(first, BANK)
             cols = slice(j * P, (j + 1) * P)
             nc.tensor.matmul_mx(
-                out=down_acc[half, j][:],
+                out=down_acc[first, count, j][:, 0:count],
                 lhsT=codes[:, cols].bitcast(FP8X4),
                 lhsT_scale=plane[:, cols],
-                rhs=v_codes[a, half][:].bitcast(FP8X4),
-                rhs_scale=v_plane[4 * a : P, half * BANK : (half + 1) * BANK],
+                rhs=v_codes[a, half][:, inner : inner + count].bitcast(FP8X4),
+                rhs_scale=v_plane[4 * a : P, first : first + count],
                 start=(a == 0),
                 stop=(a == PASSES - 1),
             )
 
-        down = {}
+        down = {(half, j): tile(f"down{half}_{j}", [P, BANK], F32) for half in range(2) for j in range(PACK)}
 
-        def copy_down(half, j):
-            down[half, j] = tile(f"down{half}_{j}", [P, BANK], F32)
-            nc.scalar.copy(down[half, j][:], down_acc[half, j][:])
+        def copy_down(first, count, j):
+            half, inner = divmod(first, BANK)
+            nc.scalar.copy(down[half, j][:, inner : inner + count], down_acc[first, count, j][:, 0:count])
 
         for a in range(PASSES):
-            for half, j in early:
-                down_pass(half, j, a)
-        for half, j in early[: len(late)]:
-            copy_down(half, j)
-        for i, (half, j) in enumerate(late):
-            down_acc[half, j] = bank(f"down_acc{half}_{j}", i)
+            for key in early:
+                down_pass(*key, a)
+        for key in early[: len(late)]:
+            copy_down(*key)
+        for i, key in enumerate(late):
+            down_acc[key] = bank(f"down_acc{key[0]}_{key[2]}", i)
             for a in range(PASSES):
-                down_pass(half, j, a)
-        for half, j in early[len(late) :] + late:
-            copy_down(half, j)
+                down_pass(*key, a)
+        for key in early[len(late) :] + late:
+            copy_down(*key)
 
-        h_f32 = {}
-        h_grouped = {piece: tile(f"h_grouped{piece}", [P, count * PACK], BF16) for piece, (first, count) in PIECES.items()}
+        h_f32 = {
+            piece: tile(f"h_f32{piece}", [P, (PACK + (piece == "B")) * count], F32)
+            for piece, (first, count) in PIECES.items()
+        }
+        h_grouped = {}
         h_q = {}
 
-        def scale_down(dst, j, first, count):
-            half, inner = divmod(first, BANK)
-            nc.vector.tensor_tensor(
-                dst, g_tab[j][:].indirect(picks(first, count)), down[half, j][:, inner : inner + count], MULT
-            )
-
-        def round_h(piece, pair, copy):
-            grouped, raw = interleaved_views(h_grouped[piece][:], h_f32[piece, pair])
-            copy(grouped[:, :, 2 * pair : 2 * pair + 2, :], raw)
-
-        def quantize_h(piece, over=None):
-            h_q[piece] = quantize(f"h{piece}", h_grouped[piece], PIECES[piece][1], over)
-
-        first_pairs = [tile(f"h_first{half}", [P, 2, BANK], F32) for half in range(2)]
-        for j in range(2):
-            for half in range(2):
-                scale_down(first_pairs[half][:, j, :], j, half * BANK, BANK)
-        for piece, (first, count) in PIECES.items():
-            half, inner = divmod(first, BANK)
-            h_f32[piece, 0] = first_pairs[half][:, :, inner : inner + count]
-            round_h(piece, 0, nc.scalar.copy)
-
-        def second_pair(piece, j, over=None):
+        def scale_down(piece, j, cuts=1):
             first, count = PIECES[piece]
-            if j == 2:
-                h_f32[piece, 1] = tile(f"h_second{piece}", [P, 2, count], F32, over)[:]
-            scale_down(h_f32[piece, 1][:, j - 2, :], j, first, count)
+            half, inner = divmod(first, BANK)
+            part = count // cuts
+            for at in range(0, count, part):
+                nc.vector.tensor_tensor(
+                    h_f32[piece][:, j * count + at : j * count + at + part],
+                    g_tab[j][:].indirect(picks(first + at, part)),
+                    down[half, j][:, inner + at : inner + at + part],
+                    MULT,
+                )
+
+        def round_h(piece, slots, copy, cuts=1, over=None, skip=0):
+            count = PIECES[piece][1]
+            if piece not in h_grouped:
+                h_grouped[piece] = tile(f"h_grouped{piece}", [P, count * PACK], BF16, over, skip)
+            planes = h_f32[piece][:, 0 : PACK * count].rearrange("p (j n) -> p j n", j=PACK)
+            grouped, raw = interleaved_views(h_grouped[piece][:], planes)
+            part = count // cuts // 4
+            for at in range(0, count // 4, part):
+                copy(grouped[:, at : at + part, slots, :], raw[:, at : at + part, slots, :])
+
+        def quantize_h(piece, cuts=1):
+            h_q[piece] = quantize(f"h{piece}", h_grouped[piece], PIECES[piece][1], cuts)
+
+        for j in range(2):
+            for piece in PIECES:
+                scale_down(piece, j)
+        round_h("A", slice(0, 2), nc.scalar.copy)
 
         wb_q = {}
         wb_grouped = {}
 
-        def round_wb(c, copy, over=None):
-            wb_grouped[c] = tile(f"wb_grouped{c}", [P, WB_COLS * PACK], BF16, over)
-            copy(*interleaved_views(wb_grouped[c][:], wb_raw[c][:]))
+        def round_wb(c, copy, grouped=None):
+            if grouped is None:
+                grouped = tile(f"wb_grouped{c}", [P, WB_COLS * PACK], BF16)[:]
+            wb_grouped[c] = grouped
+            copy(*interleaved_views(wb_grouped[c], wb_raw[c]))
 
         def quantize_wb(c):
             wb_q[c] = quantize(f"wb{c}", wb_grouped[c], WB_COLS)
@@ -308,49 +329,56 @@ def tile_list_lora_cached_projection_kernel(
             )
 
         prefilled = [("A", (n,)) for n in range(4)] + [(piece, rows) for piece in "BC" for rows in ((0, 1), (2, 3))]
-        banks = dict(zip(prefilled, [5, 6, 7, 3, 4, 0, 1, 2]))
-        second_pair("A", 2)
+        banks = dict(zip(prefilled, [6, 7, 3, 4, 5, 0, 1, 2]))
+        scale_down("A", 2)
+        scale_down("B", 2)
         for key in prefilled:
             base_passes(*key, 0, banks[key])
         for key in prefilled:
             base_passes(*key, 1)
-        round_wb(0, nc.scalar.copy)
-        second_pair("A", 3)
-        round_wb(1, nc.scalar.copy)
-        round_h("A", 1, nc.vector.tensor_copy)
-        quantize_h("A")
+        late_b = h_f32["B"][:, 3 * 256 :].bitcast(BF16)
+        late_c = h_f32["C"][:, 2 * 256 :].bitcast(BF16)
+        round_wb(0, nc.scalar.copy, late_b)
+        round_wb(1, nc.scalar.copy, late_c)
+        scale_down("A", 3, 2)
+        round_h("A", slice(2, 4), nc.vector.tensor_copy, 2)
+        quantize_h("A", 2)
         quantize_wb(0)
+        scale_down("B", 3)
         quantize_wb(1)
         for n in range(2):
             finish("A", (n,), True, "wb_raw1", n * BANK * 4)
-        round_wb(2, nc.vector.tensor_copy, "wb_grouped1")
-        round_wb(3, nc.vector.tensor_copy)
+        round_h("B", slice(0, 4), nc.vector.tensor_copy, 1, "wb_raw1", 2 * BANK * 4)
+        round_wb(2, nc.vector.tensor_copy, late_c)
+        quantize_h("B")
         quantize_wb(2)
-        quantize_wb(3)
-        second_pair("B", 2, "wb_raw3")
         for n in range(2, 4):
             finish("A", (n,))
-        for n in range(4, 8):
+        for n in range(4, 6):
             both_base_passes("A", (n,), banks["A", (n - 4,)])
-            finish("A", (n,))
-        second_pair("B", 3)
-        round_h("B", 1, nc.vector.tensor_copy)
-        quantize_h("B")
-        second_pair("C", 2, "h_groupedB")
         for rows in ((0, 1), (2, 3)):
             finish("B", rows)
-        both_base_passes("B", (4, 5), banks["A", (0,)])
-        finish("B", (4, 5))
-        second_pair("C", 3)
-        round_h("C", 1, nc.vector.tensor_copy)
-        quantize_h("C")
-        both_base_passes("B", (6, 7), banks["A", (1,)])
-        finish("B", (6, 7), False)
-        both_base_passes("C", (4, 5), banks["A", (2,)])
+        for n in range(4, 6):
+            finish("A", (n,))
+        round_wb(3, nc.vector.tensor_copy)
+        scale_down("C", 2)
+        quantize_wb(3)
+        scale_down("C", 3, 2)
+        round_h("C", slice(0, 4), nc.vector.tensor_copy, 2)
+        quantize_h("C", 2)
+        for n in range(6, 8):
+            both_base_passes("A", (n,), banks["A", (n - 4,)])
+        for n in range(6, 8):
+            finish("A", (n,))
+        both_base_passes("B", (4, 5), banks["B", (0, 1)])
+        finish("B", (4, 5), False)
         finish("C", (0, 1), False)
         finish("C", (2, 3))
+        both_base_passes("B", (6, 7), banks["B", (2, 3)])
+        finish("B", (6, 7), False)
+        both_base_passes("C", (4, 5), banks["A", (0,)])
         finish("C", (4, 5))
-        both_base_passes("C", (6,), banks["A", (3,)])
+        both_base_passes("C", (6,), banks["A", (1,)])
         finish("C", (6,), False)
-        both_base_passes("C", (7,), banks["B", (0, 1)])
-        finish("C", (7,), False)
+        both_base_passes("C", (7,), banks["A", (2,)])
+        finish("C", (7,))

@@ -28,6 +28,7 @@ N_TILES = N // P
 WB_COLS = 256
 WA_ON_SCALAR = (72, 60)
 PIECES = {"A": (0, 512), "B": (512, 256), "C": (768, 256)}
+SPANS = dict(PIECES, BC=(512, 512))
 
 
 def tile_list_lora_cached_projection_kernel(
@@ -141,17 +142,16 @@ def tile_list_lora_cached_projection_kernel(
                 raw.rearrange("p j (c i) -> p c j i", i=4),
             )
 
-        def quantize(name, grouped, cols, cuts=1):
-            codes = tile(name + "_codes", [P, cols], U32)
-            plane = tile(name + "_plane", [P, cols], U8)
-            count = cols // cuts
-            for first in range(0, cols, count):
-                nc.vector.quantize_mx(
-                    out=codes[:, first : first + count].bitcast(FP8X4),
-                    scales=plane[:, first : first + count],
-                    in_=grouped[:, first * PACK : (first + count) * PACK],
-                )
-            return codes, plane
+        def mx_tiles(name, cols):
+            return tile(name + "_codes", [P, cols], U32), tile(name + "_plane", [P, cols], U8)
+
+        def quantize(operand, grouped, first, last):
+            codes, plane = operand
+            nc.vector.quantize_mx(
+                out=codes[:, first:last].bitcast(FP8X4),
+                scales=plane[:, first:last],
+                in_=grouped[:, first * PACK : last * PACK],
+            )
 
         v_codes = {}
 
@@ -182,9 +182,10 @@ def tile_list_lora_cached_projection_kernel(
         gather_words(0, 0, "scale_rows")
         gather_words(0, 1, "tab_planes")
         round_wa(0, slice(WA_ON_SCALAR[0], P), nc.vector.tensor_copy)
-        wa_q = [quantize("wa0", wa_grouped[0], R)]
+        wa_q = [mx_tiles(f"wa{a}", R) for a in range(PASSES)]
+        quantize(wa_q[0], wa_grouped[0], 0, R)
         round_wa(1, slice(WA_ON_SCALAR[1], P), nc.vector.tensor_copy)
-        wa_q.append(quantize("wa1", wa_grouped[1], R))
+        quantize(wa_q[1], wa_grouped[1], 0, R)
         gather_words(1, 0, "wa_grouped1", 0, 2)
         gather_words(1, 1, "wa_grouped1", BANK * 4)
 
@@ -224,65 +225,67 @@ def tile_list_lora_cached_projection_kernel(
         for key in early[len(late) :] + late:
             copy_down(*key)
 
-        h_f32 = {
-            piece: tile(f"h_f32{piece}", [P, (PACK + (piece == "B")) * count], F32)
-            for piece, (first, count) in PIECES.items()
-        }
+        pitch = {"A": 512, "B": 256, "C": 256}
+        h_f32 = {piece: tile(f"h_f32{piece}", [P, (PACK + (piece == "B")) * pitch[piece]], F32) for piece in PIECES}
         h_grouped = {}
-        h_q = {}
+        h_q = {span: [t[:] for t in mx_tiles(f"h{span}", BANK)] for span in ("A", "BC")}
+        h_q["B"] = [t[:, 0:256] for t in h_q["BC"]]
+        h_q["C"] = [t[:, 256:512] for t in h_q["BC"]]
 
-        def scale_down(piece, j, cuts=1):
+        def scale_down(piece, j, *cuts):
             first, count = PIECES[piece]
             half, inner = divmod(first, BANK)
-            part = count // cuts
-            for at in range(0, count, part):
+            for at, end in zip((0,) + cuts, cuts + (count,)):
+                part = end - at
                 nc.vector.tensor_tensor(
-                    h_f32[piece][:, j * count + at : j * count + at + part],
+                    h_f32[piece][:, j * pitch[piece] + at : j * pitch[piece] + at + part],
                     g_tab[j][:].indirect(picks(first + at, part)),
                     down[half, j][:, inner + at : inner + at + part],
                     MULT,
                 )
 
-        def round_h(piece, slots, copy, cuts=1, over=None, skip=0):
+        def round_h(piece, slots, copy, *ranges):
             count = PIECES[piece][1]
+            if piece == "B":
+                h_grouped[piece] = tile("h_groupedB", [P, count * PACK], BF16, "wb_raw1", 2 * BANK * 4)
             if piece not in h_grouped:
-                h_grouped[piece] = tile(f"h_grouped{piece}", [P, count * PACK], BF16, over, skip)
+                h_grouped[piece] = tile(f"h_grouped{piece}", [P, count * PACK], BF16)
             planes = h_f32[piece][:, 0 : PACK * count].rearrange("p (j n) -> p j n", j=PACK)
             grouped, raw = interleaved_views(h_grouped[piece][:], planes)
-            part = count // cuts // 4
-            for at in range(0, count // 4, part):
-                copy(grouped[:, at : at + part, slots, :], raw[:, at : at + part, slots, :])
+            for first, last in ranges:
+                copy(grouped[:, first // 4 : last // 4, slots, :], raw[:, first // 4 : last // 4, slots, :])
 
-        def quantize_h(piece, cuts=1):
-            h_q[piece] = quantize(f"h{piece}", h_grouped[piece], PIECES[piece][1], cuts)
+        def quantize_h(piece, first, last):
+            quantize(h_q[piece], h_grouped[piece], first, last)
 
         for j in range(2):
             for piece in PIECES:
                 scale_down(piece, j)
-        round_h("A", slice(0, 2), nc.scalar.copy)
+        round_h("A", slice(0, 2), nc.scalar.copy, (0, 512))
 
-        wb_q = {}
-        wb_grouped = {}
+        wb_q = [mx_tiles(f"wb{c}", WB_COLS) for c in range(N // WB_COLS)]
+        wb_grouped = {3: tile("wb_grouped3", [P, WB_COLS * PACK], BF16)[:]}
+        wb_grouped[0] = h_f32["B"][:, 3 * 256 :].bitcast(BF16)
+        wb_grouped[1] = h_f32["C"][:, 2 * 256 :].bitcast(BF16)
+        wb_grouped[2] = wb_grouped[1]
 
-        def round_wb(c, copy, grouped=None):
-            if grouped is None:
-                grouped = tile(f"wb_grouped{c}", [P, WB_COLS * PACK], BF16)[:]
-            wb_grouped[c] = grouped
-            copy(*interleaved_views(wb_grouped[c], wb_raw[c]))
+        def round_wb(c, copy, first=0, last=WB_COLS):
+            grouped, raw = interleaved_views(wb_grouped[c], wb_raw[c])
+            copy(grouped[:, first // 4 : last // 4], raw[:, first // 4 : last // 4])
 
         def quantize_wb(c):
-            wb_q[c] = quantize(f"wb{c}", wb_grouped[c], WB_COLS)
+            quantize(wb_q[c], wb_grouped[c], 0, WB_COLS)
 
         y_acc = {}
 
         def columns(piece, rows, n):
-            count = PIECES[piece][1]
+            count = SPANS[piece][1]
             return slice((n - rows[0]) * count, (n - rows[0] + 1) * count)
 
         def base_passes(piece, rows, a, number=None):
             if a == 0:
                 y_acc[piece, rows] = bank(f"y_acc{piece}{rows[0]}", number)
-            first, count = PIECES[piece]
+            first, count = SPANS[piece]
             half, inner = divmod(first, BANK)
             scales = v_plane[:] if a == 0 else moved_plane[:].bitcast(U8)
             for n in rows:
@@ -301,21 +304,26 @@ def tile_list_lora_cached_projection_kernel(
             base_passes(piece, rows, 0, number)
             base_passes(piece, rows, 1)
 
-        def finish(piece, rows, on_scalar=True, over=None, skip=0):
-            first, count = PIECES[piece]
-            acc = y_acc[piece, rows]
+        def close(piece, rows, first=0, last=None):
+            count = SPANS[piece][1]
+            last = last or count
             for n in rows:
                 c, col = divmod(n * P, WB_COLS)
                 codes, plane = wb_q[c]
                 nc.tensor.matmul_mx(
-                    out=acc[:, columns(piece, rows, n)],
+                    out=y_acc[piece, rows][:, columns(piece, rows, n)][:, first:last],
                     lhsT=codes[:, col : col + P].bitcast(FP8X4),
                     lhsT_scale=plane[:, col : col + P],
-                    rhs=h_q[piece][0][:].bitcast(FP8X4),
-                    rhs_scale=h_q[piece][1][:],
+                    rhs=h_q[piece][0][:, first:last].bitcast(FP8X4),
+                    rhs_scale=h_q[piece][1][:, first:last],
                     start=False,
-                    stop=(n == rows[-1]),
+                    stop=(n == rows[-1] and last == count),
                 )
+
+        def finish(piece, rows, on_scalar=True, over=None, skip=0, first_open=0):
+            close(piece, rows, first_open)
+            first, count = SPANS[piece]
+            acc = y_acc[piece, rows]
             result = tile(f"result{piece}{rows[0]}", [P, len(rows) * count], F32, over, skip)
             for n in rows:
                 cols = columns(piece, rows, n)
@@ -336,21 +344,20 @@ def tile_list_lora_cached_projection_kernel(
             base_passes(*key, 0, banks[key])
         for key in prefilled:
             base_passes(*key, 1)
-        late_b = h_f32["B"][:, 3 * 256 :].bitcast(BF16)
-        late_c = h_f32["C"][:, 2 * 256 :].bitcast(BF16)
-        round_wb(0, nc.scalar.copy, late_b)
-        round_wb(1, nc.scalar.copy, late_c)
-        scale_down("A", 3, 2)
-        round_h("A", slice(2, 4), nc.vector.tensor_copy, 2)
-        quantize_h("A", 2)
+        round_wb(0, nc.scalar.copy)
+        round_wb(1, nc.scalar.copy)
+        scale_down("A", 3, 256)
+        round_h("A", slice(2, 4), nc.vector.tensor_copy, (0, 256), (256, 512))
+        quantize_h("A", 0, 256)
+        quantize_h("A", 256, 512)
         quantize_wb(0)
         scale_down("B", 3)
         quantize_wb(1)
         for n in range(2):
             finish("A", (n,), True, "wb_raw1", n * BANK * 4)
-        round_h("B", slice(0, 4), nc.vector.tensor_copy, 1, "wb_raw1", 2 * BANK * 4)
-        round_wb(2, nc.vector.tensor_copy, late_c)
-        quantize_h("B")
+        round_h("B", slice(0, 4), nc.vector.tensor_copy, (0, 256))
+        round_wb(2, nc.vector.tensor_copy)
+        quantize_h("B", 0, 256)
         quantize_wb(2)
         for n in range(2, 4):
             finish("A", (n,))
@@ -363,22 +370,21 @@ def tile_list_lora_cached_projection_kernel(
         round_wb(3, nc.vector.tensor_copy)
         scale_down("C", 2)
         quantize_wb(3)
-        scale_down("C", 3, 2)
-        round_h("C", slice(0, 4), nc.vector.tensor_copy, 2)
-        quantize_h("C", 2)
+        scale_down("C", 3, 128)
+        round_h("C", slice(0, 4), nc.vector.tensor_copy, (0, 128), (128, 256))
+        quantize_h("C", 0, 128)
+        quantize_h("C", 128, 256)
         for n in range(6, 8):
             both_base_passes("A", (n,), banks["A", (n - 4,)])
         for n in range(6, 8):
             finish("A", (n,))
-        both_base_passes("B", (4, 5), banks["B", (0, 1)])
-        finish("B", (4, 5), False)
+        freed = [banks["B", (0, 1)], banks["B", (2, 3)], banks["A", (0,)], banks["A", (1,)]]
+        for n in range(4, 6):
+            both_base_passes("BC", (n,), freed[n - 4])
         finish("C", (0, 1), False)
         finish("C", (2, 3))
-        both_base_passes("B", (6, 7), banks["B", (2, 3)])
-        finish("B", (6, 7), False)
-        both_base_passes("C", (4, 5), banks["A", (0,)])
-        finish("C", (4, 5))
-        both_base_passes("C", (6,), banks["A", (1,)])
-        finish("C", (6,), False)
-        both_base_passes("C", (7,), banks["A", (2,)])
-        finish("C", (7,))
+        finish("BC", (4,), False)
+        finish("BC", (5,))
+        for n in range(6, 8):
+            both_base_passes("BC", (n,), freed[n - 4])
+            finish("BC", (n,), n % 2 == 1)

@@ -216,13 +216,12 @@ def tile_list_lora_cached_projection_kernel(
         for a in range(PASSES):
             for key in early:
                 down_pass(*key, a)
-        for key in early[: len(late)]:
+        for key in early:
             copy_down(*key)
-        for i, key in enumerate(late):
-            down_acc[key] = bank(f"down_acc{key[0]}_{key[2]}", i)
+        for number, key in zip((0, 5, 0), late):
+            down_acc[key] = bank(f"down_acc{key[0]}_{key[2]}", number)
             for a in range(PASSES):
                 down_pass(*key, a)
-        for key in early[len(late) :] + late:
             copy_down(*key)
 
         pitch = {"A": 512, "B": 256, "C": 256}
@@ -337,7 +336,7 @@ def tile_list_lora_cached_projection_kernel(
             )
 
         prefilled = [("A", (n,)) for n in range(4)] + [(piece, rows) for piece in "BC" for rows in ((0, 1), (2, 3))]
-        banks = dict(zip(prefilled, [6, 7, 3, 4, 5, 0, 1, 2]))
+        banks = dict(zip(prefilled, [6, 7, 1, 2, 3, 4, 5, 0]))
         scale_down("A", 2)
         scale_down("B", 2)
         for key in prefilled:
@@ -378,13 +377,14 @@ def tile_list_lora_cached_projection_kernel(
             both_base_passes("A", (n,), banks["A", (n - 4,)])
         for n in range(6, 8):
             finish("A", (n,))
-        freed = [banks["B", (0, 1)], banks["B", (2, 3)], banks["A", (0,)], banks["A", (1,)]]
-        for n in range(4, 6):
-            both_base_passes("BC", (n,), freed[n - 4])
+        both_base_passes("BC", (4,), banks["B", (0, 1)])
         finish("C", (0, 1), False)
-        finish("C", (2, 3))
-        finish("BC", (4,), False)
-        finish("BC", (5,))
-        for n in range(6, 8):
-            both_base_passes("BC", (n,), freed[n - 4])
-            finish("BC", (n,), n % 2 == 1)
+        finish("C", (2, 3), False)
+        finish("BC", (4,))
+        for n, number in ((5, banks["B", (2, 3)]), (6, banks["A", (0,)])):
+            both_base_passes("BC", (n,), number)
+            finish("BC", (n,), n % 2 == 0)
+        both_base_passes("B", (7,), banks["A", (1,)])
+        finish("B", (7,), False)
+        both_base_passes("C", (7,), banks["A", (2,)])
+        finish("C", (7,), False)

@@ -42,8 +42,9 @@ def tile_list_lora_cached_projection_kernel(
 
         place = {"end": 0}
 
-        def tile(name, shape, dtype, over=None, skip=0):
+        def tile(name, shape, dtype, over=None, skip=0, quarter=0):
             if over is None:
+                place["end"] += (64 * quarter - place["end"]) % 256
                 place[name] = place["end"]
                 place["end"] += math.prod(shape[1:]) * ELEMENT_BYTES[dtype]
             else:
@@ -69,9 +70,9 @@ def tile_list_lora_cached_projection_kernel(
         nc.sync.dma_start(out=bias_rows[0:N_TILES, :], in_=bias.rearrange("(c p) -> c p", p=P))
         tab_planes = tile("tab_planes", [P, T // 4], I32)
         nc.vector.memset(tab_planes[:], 0)
-        w4_planes = tile("w4_planes", [P, PASSES, N // 4], I32)
+        w4_planes = tile("w4_planes", [P, PASSES, N // 4], I32, quarter=3)
         nc.vector.memset(w4_planes[:], 0)
-        moved_plane = tile("moved_plane", [P, S // 4], I32)
+        moved_plane = tile("moved_plane", [P, S // 4], I32, quarter=2)
         nc.vector.memset(moved_plane[:], 0)
         for q in range(4):
             nc.vector.tensor_copy(tab_planes[32 * q : 32 * q + 8, :], scale_rows[32 * q : 32 * q + 8, :])
@@ -80,7 +81,7 @@ def tile_list_lora_cached_projection_kernel(
 
         tab_w = [tile(f"tab_w{a}", [P, T], I32) for a in range(PASSES)]
         wa_raw = [tile(f"wa_raw{a}", [P, PACK, R], F32) for a in range(PASSES)]
-        w4_codes = [tile(f"w4_codes{u}", [P, PASSES, N], U8) for u in range(2)]
+        w4_codes = [tile(f"w4_codes{u}", [P, PASSES, N], U8, quarter=1) for u in range(2)]
         g_tab = [tile(f"g_tab{j}", [P, T], F32) for j in range(PACK)]
         wb_raw = [
             tile(f"wb_raw{c}", [P, PACK + (2 if c == 1 else 0), WB_COLS], F32)[:, 0:PACK, :] for c in range(N // WB_COLS)
@@ -115,7 +116,7 @@ def tile_list_lora_cached_projection_kernel(
         load_wa(1)
         load_words(1)
 
-        v_plane = tile("v_plane", [P, S], U8)
+        v_plane = tile("v_plane", [P, S], U8, quarter=2)
         nc.vector.tensor_copy(v_plane[:], tab_planes[:].bitcast(U8).indirect(offsets[:]))
 
         load_g(0)
@@ -142,8 +143,11 @@ def tile_list_lora_cached_projection_kernel(
                 raw.rearrange("p j (c i) -> p c j i", i=4),
             )
 
-        def mx_tiles(name, cols):
-            return tile(name + "_codes", [P, cols], U32), tile(name + "_plane", [P, cols], U8)
+        def mx_tiles(name, cols, stationary=1):
+            return (
+                tile(name + "_codes", [P, cols], U32, quarter=stationary),
+                tile(name + "_plane", [P, cols], U8, quarter=2 + stationary),
+            )
 
         def quantize(operand, grouped, first, last):
             codes, plane = operand
@@ -227,7 +231,7 @@ def tile_list_lora_cached_projection_kernel(
         pitch = {"A": 512, "B": 256, "C": 256}
         h_f32 = {piece: tile(f"h_f32{piece}", [P, (PACK + (piece == "B")) * pitch[piece]], F32) for piece in PIECES}
         h_grouped = {}
-        h_q = {span: [t[:] for t in mx_tiles(f"h{span}", BANK)] for span in ("A", "BC")}
+        h_q = {span: [t[:] for t in mx_tiles(f"h{span}", BANK, 0)] for span in ("A", "BC")}
         h_q["B"] = [t[:, 0:256] for t in h_q["BC"]]
         h_q["C"] = [t[:, 256:512] for t in h_q["BC"]]
 

import math
from contextlib import ExitStack

import concourse.mybir as mybir
from concourse.masks import make_identity

K, R, N, T, S = 1024, 512, 1024, 2048, 1024
FLOPS = 2 * S * (K * R + K * N + R * N)

F32 = mybir.dt.float32
BF16 = mybir.dt.bfloat16
I32 = mybir.dt.int32
U32 = mybir.dt.uint32
U16 = mybir.dt.uint16
U8 = mybir.dt.uint8
FP8X4 = mybir.dt.float8_e4m3fn_x4
FP4X4 = mybir.dt.float4_e2m1fn_x4
MULT = mybir.AluOpType.mult
ADD = mybir.AluOpType.add
IDENTITY = mybir.ActivationFunctionType.Identity
ELEMENT_BYTES = {F32: 4, I32: 4, U32: 4, BF16: 2, U8: 1}

P = 128
PACK = 4
PASSES = K // (P * PACK)
BANK = 512
N_TILES = N // P
WB_COLS = 256
WA_ON_SCALAR = (72, 60)
PIECES = {"A": (0, 512), "B": (512, 256), "C": (768, 256)}
SPANS = dict(PIECES, BC=(512, 512))


def tile_list_lora_cached_projection_kernel(
    tc, tab_words, tab_scales, offs, gT, w4_words, w4_scales, wa, wb, bias, out
):
    nc = tc.nc
    with ExitStack() as ctx:
        lists = ctx.enter_context(tc.tile_pool(name="lists", bufs=1))
        sbuf = ctx.enter_context(tc.tile_pool(name="sbuf", bufs=1))
        psum = ctx.enter_context(tc.psum_pool(name="psum", bufs=1))

        place = {"end": 0}

        def tile(name, shape, dtype, over=None, skip=0, quarter=0):
            if over is None:
                place["end"] += (64 * quarter - place["end"]) % 256
                place[name] = place["end"]
                place["end"] += math.prod(shape[1:]) * ELEMENT_BYTES[dtype]
            else:
                place[name] = place[over] + skip
            return sbuf.tile(shape, dtype, name=name, offset=place[name], align_bytes=64)

        def bank(name, number):
            return psum.tile([P, BANK], F32, name=name, tag=f"bank{number}")

        offsets = lists.tile([P, S // 16], U16, name="offsets")

        def picks(first, count):
            return offsets[:, first // 16 : (first + count) // 16]

        scale_rows = tile("scale_rows", [P, T // 4], I32)
        for q in range(4):
            nc.sync.dma_start(
                out=scale_rows[32 * q : 32 * q + 8, :], in_=tab_scales[:, 4 * q : 4 * q + 4, :].bitcast(I32)
            )
        nc.sync.dma_start(offsets[:], offs)
        bias_rows = tile("bias_rows", [P, P], F32)
        nc.gpsimd.memset(bias_rows[:], 0.0)
        nc.sync.dma_start(out=bias_rows[0:N_TILES, :], in_=bias.rearrange("(c p) -> c p", p=P))
        tab_planes = tile("tab_planes", [P, T // 4], I32)
        nc.vector.memset(tab_planes[:], 0)
        w4_planes = tile("w4_planes", [P, PASSES, N // 4], I32, quarter=3)
        nc.vector.memset(w4_planes[:], 0)
        moved_plane = tile("moved_plane", [P, S // 4], I32, quarter=2)
        nc.vector.memset(moved_plane[:], 0)
        for q in range(4):
            nc.vector.tensor_copy(tab_planes[32 * q : 32 * q + 8, :], scale_rows[32 * q : 32 * q + 8, :])
        identity = tile("identity", [P, P], F32)
        make_identity(nc, identity[:])

        tab_w = [tile(f"tab_w{a}", [P, T], I32) for a in range(PASSES)]
        wa_raw = [tile(f"wa_raw{a}", [P, PACK, R], F32) for a in range(PASSES)]
        w4_codes = [tile(f"w4_codes{u}", [P, PASSES, N], U8, quarter=1) for u in range(2)]
        g_tab = [tile(f"g_tab{j}", [P, T], F32) for j in range(PACK)]
        wb_raw = [
            tile(f"wb_raw{c}", [P, PACK + (2 if c == 1 else 0), WB_COLS], F32)[:, 0:PACK, :] for c in range(N // WB_COLS)
        ]

        def load_words(a):
            nc.sync.dma_start(out=tab_w[a][:], in_=tab_words[a].rearrange("p t i -> p (t i)").bitcast(I32))

        def load_wa(a):
            nc.sync.dma_start(
                out=wa_raw[a][:],
                in_=wa[a * P * PACK : (a + 1) * P * PACK, :].rearrange("(p j) r -> p j r", j=PACK),
            )

        def load_w4(u):
            nc.sync.dma_start(
                out=w4_codes[u][:].bitcast(I32),
                in_=w4_words[:, :, u * N : (u + 1) * N].rearrange("a p b -> p a b").bitcast(I32),
            )

        def load_wb(c):
            nc.sync.dma_start(
                out=wb_raw[c],
                in_=wb[:, c * WB_COLS : (c + 1) * WB_COLS].rearrange("(p j) n -> p j n", j=PACK),
            )

        def load_g(j):
            nc.sync.dma_start(out=g_tab[j][:], in_=gT.rearrange("(p j) t -> j p t", j=PACK)[j])

        load_words(0)
        load_wa(0)
        load_wa(1)
        load_words(1)

        v_plane = tile("v_plane", [P, S], U8, quarter=2)
        nc.vector.tensor_copy(v_plane[:], tab_planes[:].bitcast(U8).indirect(offsets[:]))

        load_g(0)
        for r in range(4):
            nc.sync.dma_start(
                out=w4_planes[r:P:32, :, :],
                in_=w4_scales[:, r:16:4, :].rearrange("a q c -> q a c").bitcast(I32),
            )
        load_g(1)
        load_g(2)
        load_w4(0)
        load_g(3)
        for r in range(4):
            nc.sync.dma_start(out=moved_plane[r:P:32, :], in_=v_plane[4 + r : P : 32, :].bitcast(I32))
        load_wb(0)
        load_wb(1)
        load_wb(2)
        load_w4(1)
        load_wb(3)

        def interleaved_views(grouped, raw):
            return (
                grouped.rearrange("p (c i j) -> p c j i", i=4, j=PACK),
                raw.rearrange("p j (c i) -> p c j i", i=4),
            )

        def mx_tiles(name, cols, stationary=1):
            return (
                tile(name + "_codes", [P, cols], U32, quarter=stationary),
                tile(name + "_plane", [P, cols], U8, quarter=2 + stationary),
            )

        def quantize(operand, grouped, first, last):
            codes, plane = operand
            nc.vector.quantize_mx(
                out=codes[:, first:last].bitcast(FP8X4),
                scales=plane[:, first:last],
                in_=grouped[:, first * PACK : last * PACK],
            )

        v_codes = {}

        def gather_words(a, half, over, skip=0, cuts=1):
            v_codes[a, half] = tile(f"v_codes{a}_{half}", [P, BANK], U32, over, skip)
            count = BANK // cuts
            for inner in range(0, BANK, count):
                nc.vector.tensor_copy(
                    v_codes[a, half][:, inner : inner + count],
                    tab_w[a][:].bitcast(U32).indirect(picks(half * BANK + inner, count)),
                )

        wa_grouped = [tile(f"wa_grouped{a}", [P, R * PACK], BF16) for a in range(PASSES)]

        def round_wa(a, columns, copy):
            copy(
                wa_grouped[a][:].rearrange("p (t m j) -> p m j t", t=PACK, j=PACK)[:, columns],
                wa_raw[a][:].rearrange("p j (m t) -> p m j t", t=PACK)[:, columns],
            )

        round_wa(0, slice(0, WA_ON_SCALAR[0]), nc.scalar.copy)
        bias_bank = bank("bias_bank", N_TILES - 1)
        nc.tensor.transpose(bias_bank[:, 0:P], bias_rows[:], identity[:])
        bias_cols = tile("bias_cols", [P, 2 * N_TILES], F32)
        nc.scalar.activation(bias_cols[:, 0:N_TILES], bias_bank[:, 0:N_TILES], IDENTITY)
        round_wa(1, slice(0, WA_ON_SCALAR[1]), nc.scalar.copy)

        gather_words(0, 0, "scale_rows")
        gather_words(0, 1, "tab_planes")
        round_wa(0, slice(WA_ON_SCALAR[0], P), nc.vector.tensor_copy)
        wa_q = [mx_tiles(f"wa{a}", R) for a in range(PASSES)]
        quantize(wa_q[0], wa_grouped[0], 0, R)
        round_wa(1, slice(WA_ON_SCALAR[1], P), nc.vector.tensor_copy)
        quantize(wa_q[1], wa_grouped[1], 0, R)
        gather_words(1, 0, "wa_grouped1", 0, 2)
        gather_words(1, 1, "wa_grouped1", BANK * 4)

        early = [(0, 256, 0), (256, 256, 0), (512, 512, 0), (0, 512, 1), (512, 512, 1), (0, 512, 2)]
        late = [(0, 512, 3), (512, 512, 2), (512, 512, 3)]
        down_acc = {key: bank(f"down_acc{key[0]}_{key[2]}", i) for i, key in enumerate(early)}

        def down_pass(first, count, j, a):
            codes, plane = wa_q[a]
            half, inner = divmod(first, BANK)
            cols = slice(j * P, (j + 1) * P)
            nc.tensor.matmul_mx(
                out=down_acc[first, count, j][:, 0:count],
                lhsT=codes[:, cols].bitcast(FP8X4),
                lhsT_scale=plane[:, cols],
                rhs=v_codes[a, half][:, inner : inner + count].bitcast(FP8X4),
                rhs_scale=v_plane[4 * a : P, first : first + count],
                start=(a == 0),
                stop=(a == PASSES - 1),
            )

        down = {(half, j): tile(f"down{half}_{j}", [P, BANK], F32) for half in range(2) for j in range(PACK)}

        def copy_down(first, count, j):
            half, inner = divmod(first, BANK)
            nc.scalar.copy(down[half, j][:, inner : inner + count], down_acc[first, count, j][:, 0:count])

        for a in range(PASSES):
            for key in early:
                down_pass(*key, a)
        for key in early:
            copy_down(*key)
        for number, key in zip((0, 5, 0), late):
            down_acc[key] = bank(f"down_acc{key[0]}_{key[2]}", number)
            for a in range(PASSES):
                down_pass(*key, a)
            copy_down(*key)

        pitch = {"A": 512, "B": 256, "C": 256}
        h_f32 = {piece: tile(f"h_f32{piece}", [P, (PACK + (piece == "B")) * pitch[piece]], F32) for piece in PIECES}
        h_grouped = {}
        h_q = {span: [t[:] for t in mx_tiles(f"h{span}", BANK, 0)] for span in ("A", "BC")}
        h_q["B"] = [t[:, 0:256] for t in h_q["BC"]]
        h_q["C"] = [t[:, 256:512] for t in h_q["BC"]]

        def scale_down(piece, j, *cuts):
            first, count = PIECES[piece]
            half, inner = divmod(first, BANK)
            for at, end in zip((0,) + cuts, cuts + (count,)):
                part = end - at
                nc.vector.tensor_tensor(
                    h_f32[piece][:, j * pitch[piece] + at : j * pitch[piece] + at + part],
                    g_tab[j][:].indirect(picks(first + at, part)),
                    down[half, j][:, inner + at : inner + at + part],
                    MULT,
                )

        def round_h(piece, slots, copy, *ranges):
            count = PIECES[piece][1]
            if piece == "B":
                h_grouped[piece] = tile("h_groupedB", [P, count * PACK], BF16, "wb_raw1", 2 * BANK * 4)
            if piece not in h_grouped:
                h_grouped[piece] = tile(f"h_grouped{piece}", [P, count * PACK], BF16)
            planes = h_f32[piece][:, 0 : PACK * count].rearrange("p (j n) -> p j n", j=PACK)
            grouped, raw = interleaved_views(h_grouped[piece][:], planes)
            for first, last in ranges:
                copy(grouped[:, first // 4 : last // 4, slots, :], raw[:, first // 4 : last // 4, slots, :])

        def quantize_h(piece, first, last):
            quantize(h_q[piece], h_grouped[piece], first, last)

        for j in range(2):
            for piece in PIECES:
                scale_down(piece, j)
        round_h("A", slice(0, 2), nc.scalar.copy, (0, 512))

        wb_q = [mx_tiles(f"wb{c}", WB_COLS) for c in range(N // WB_COLS)]
        wb_grouped = {3: tile("wb_grouped3", [P, WB_COLS * PACK], BF16)[:]}
        wb_grouped[0] = h_f32["B"][:, 3 * 256 :].bitcast(BF16)
        wb_grouped[1] = h_f32["C"][:, 2 * 256 :].bitcast(BF16)
        wb_grouped[2] = wb_grouped[1]

        def round_wb(c, copy, first=0, last=WB_COLS):
            grouped, raw = interleaved_views(wb_grouped[c], wb_raw[c])
            copy(grouped[:, first // 4 : last // 4], raw[:, first // 4 : last // 4])

        def quantize_wb(c):
            quantize(wb_q[c], wb_grouped[c], 0, WB_COLS)

        y_acc = {}

        def columns(piece, rows, n):
            count = SPANS[piece][1]
            return slice((n - rows[0]) * count, (n - rows[0] + 1) * count)

        def base_passes(piece, rows, a, number=None):
            if a == 0:
                y_acc[piece, rows] = bank(f"y_acc{piece}{rows[0]}", number)
            first, count = SPANS[piece]
            half, inner = divmod(first, BANK)
            scales = v_plane[:] if a == 0 else moved_plane[:].bitcast(U8)
            for n in rows:
                u, c = divmod(n, N_TILES // 2)
                nc.tensor.matmul_mx(
                    out=y_acc[piece, rows][:, columns(piece, rows, n)],
                    lhsT=w4_codes[u][:, a, 2 * c * P : 2 * (c + 1) * P].bitcast(FP4X4),
                    lhsT_scale=w4_planes[:, a, :].bitcast(U8)[:, n * P : (n + 1) * P],
                    rhs=v_codes[a, half][:, inner : inner + count].bitcast(FP8X4),
                    rhs_scale=scales[:, first : first + count],
                    start=(a == 0 and n == rows[0]),
                    stop=False,
                )

        def both_base_passes(piece, rows, number):
            base_passes(piece, rows, 0, number)
            base_passes(piece, rows, 1)

        def close(piece, rows, first=0, last=None):
            count = SPANS[piece][1]
            last = last or count
            for n in rows:
                c, col = divmod(n * P, WB_COLS)
                codes, plane = wb_q[c]
                nc.tensor.matmul_mx(
                    out=y_acc[piece, rows][:, columns(piece, rows, n)][:, first:last],
                    lhsT=codes[:, col : col + P].bitcast(FP8X4),
                    lhsT_scale=plane[:, col : col + P],
                    rhs=h_q[piece][0][:, first:last].bitcast(FP8X4),
                    rhs_scale=h_q[piece][1][:, first:last],
                    start=False,
                    stop=(n == rows[-1] and last == count),
                )

        def finish(piece, rows, on_scalar=True, over=None, skip=0, first_open=0):
            close(piece, rows, first_open)
            first, count = SPANS[piece]
            acc = y_acc[piece, rows]
            result = tile(f"result{piece}{rows[0]}", [P, len(rows) * count], F32, over, skip)
            for n in rows:
                cols = columns(piece, rows, n)
                if on_scalar:
                    nc.scalar.activation(result[:, cols], acc[:, cols], IDENTITY, bias=bias_cols[:, n : n + 1])
                else:
                    nc.vector.tensor_scalar(result[:, cols], acc[:, cols], bias_cols[:, n : n + 1], None, ADD)
            nc.sync.dma_start(
                out=out[rows[0] * P : (rows[-1] + 1) * P, first : first + count].rearrange("(c p) t -> p c t", p=P),
                in_=result[:].rearrange("p (c t) -> p c t", t=count),
            )

        prefilled = [("A", (n,)) for n in range(4)] + [(piece, rows) for piece in "BC" for rows in ((0, 1), (2, 3))]
        banks = dict(zip(prefilled, [6, 7, 1, 2, 3, 4, 5, 0]))
        scale_down("A", 2)
        scale_down("B", 2)
        for key in prefilled:
            base_passes(*key, 0, banks[key])
        for key in prefilled:
            base_passes(*key, 1)
        round_wb(0, nc.scalar.copy)
        round_wb(1, nc.scalar.copy)
        scale_down("A", 3, 256)
        round_h("A", slice(2, 4), nc.vector.tensor_copy, (0, 256), (256, 512))
        quantize_h("A", 0, 256)
        quantize_h("A", 256, 512)
        quantize_wb(0)
        scale_down("B", 3)
        quantize_wb(1)
        for n in range(2):
            finish("A", (n,), True, "wb_raw1", n * BANK * 4)
        round_h("B", slice(0, 4), nc.vector.tensor_copy, (0, 256))
        round_wb(2, nc.vector.tensor_copy)
        quantize_h("B", 0, 256)
        quantize_wb(2)
        for n in range(2, 4):
            finish("A", (n,))
        for n in range(4, 6):
            both_base_passes("A", (n,), banks["A", (n - 4,)])
        for rows in ((0, 1), (2, 3)):
            finish("B", rows)
        for n in range(4, 6):
            finish("A", (n,))
        round_wb(3, nc.vector.tensor_copy)
        scale_down("C", 2)
        quantize_wb(3)
        scale_down("C", 3, 128)
        round_h("C", slice(0, 4), nc.vector.tensor_copy, (0, 128), (128, 256))
        quantize_h("C", 0, 128)
        quantize_h("C", 128, 256)
        for n in range(6, 8):
            both_base_passes("A", (n,), banks["A", (n - 4,)])
        for n in range(6, 8):
            finish("A", (n,))
        both_base_passes("BC", (4,), banks["B", (0, 1)])
        finish("C", (0, 1), False)
        finish("C", (2, 3), False)
        finish("BC", (4,))
        for n, number in ((5, banks["B", (2, 3)]), (6, banks["A", (0,)])):
            both_base_passes("BC", (n,), number)
            finish("BC", (n,), n % 2 == 0)
        both_base_passes("B", (7,), banks["A", (1,)])
        finish("B", (7,), False)
        both_base_passes("C", (7,), banks["A", (2,)])
        finish("C", (7,), False)
